import numpy as np, ml_dtypes
CORES = [40,64,80,88,96,104,120,144]
N = 8
import mx_ref
BF = ml_dtypes.bfloat16
def gentries(a):
    return np.ascontiguousarray(a.reshape(8, 16, -1).transpose(0, 2, 1)).reshape(8, -1)
def gtable(e):
    e = np.asarray(e); return np.ascontiguousarray(e.reshape(8, -1, 16).transpose(0, 2, 1)).reshape(128, -1).astype(np.int32)
def gcols(t, e):
    v = np.concatenate([t.reshape(8, 16, -1, 4), np.zeros((8, 16, 1, 4), BF)], axis=2)
    return np.ascontiguousarray(np.stack([v[g][:, e[g]] for g in range(8)])).reshape(128, -1)
def gpick(z, e):
    return np.concatenate([z[16 * g:16 * g + 16][:, e[g]] for g in range(8)])
def tile(rs):
    return np.stack(rs, axis=2).reshape(128, -1).astype(BF)
def pick(q, e):
    c = np.concatenate([q[0].reshape(128, -1, 4), np.zeros((128, 1, 4), np.uint8)], axis=1); s = np.concatenate([q[1], np.ones((16, 1), np.uint8)], axis=1)
    return (np.ascontiguousarray(c[:, e].reshape(128, -1)), np.ascontiguousarray(s[:, e]))
def join(*qs):
    return (np.concatenate([q[0] for q in qs], axis=1), np.concatenate([q[1] for q in qs], axis=1))
def put(q, e, v):
    c, s = q[0].reshape(128, -1, 4).copy(), q[1].copy(); c[:, e] = v[0].reshape(128, -1, 4); s[:, e] = v[1]
    return (c.reshape(128, -1), s)
def pk(c, s):
    return (np.ascontiguousarray(c), mx_ref.live(s))
def emit(q):
    return q[0], q[1]
def packed(v, rng):
    q = [mx_ref.quantize(np.ascontiguousarray(v[r])) for r in range(N)]
    return np.stack([a for a, b in q]), np.stack([mx_ref.plane(b, rng) for a, b in q])
def values_of_codes():
    e, c = np.zeros((128, 128, 4), np.float32), np.zeros((128, 2, 4), np.uint8)
    e[np.arange(128), np.arange(128), 0] = 1
    c[:127, :, 0] = np.arange(256).reshape(2, 128).T[:127]
    return mx_ref.matmul(mx_ref.quantize(e.reshape(128, 512).astype(BF)), (c.reshape(128, 8), np.full((16, 2), 127, np.uint8))).T.reshape(-1).astype(np.float64)
CODE_VALUE, SCALE_VALUE = values_of_codes(), 2.0 ** (np.arange(256) - 127.0)
def decode(q):
    return (CODE_VALUE[q[0]].reshape(16, 8, -1, 4) * SCALE_VALUE[q[1]][:, None, :, None] + 0.0).reshape(128, -1).astype(np.float32)
def f(rng, *shape):
    return mx_ref.flush((rng.standard_normal(shape, dtype=np.float32) * np.exp2(rng.integers(-2, 3, shape[:-1] + (1,)))).astype(BF))
def wide(rng, *shape, cols=0):
    v = rng.standard_normal(shape, dtype=np.float32) * np.exp2(rng.integers(-12, 13, shape)).astype(np.float32)
    if cols: v *= np.repeat(np.exp2(rng.integers(-cols, cols + 1, shape[:-2] + (1, shape[-1] // 4))) * (rng.random(shape[:-2] + (1, shape[-1] // 4)) > 0.0625), 4, axis=-1).astype(np.float32)
    return mx_ref.flush(v.astype(BF))
C, L, M, R = 288, 4, 56, 3
def big(v):
    v = v.astype(np.float32)
    v[np.abs(v) < np.float32(2.0 ** -16)] = 0
    return v.astype(BF)
def numbers_of(rng):
    return {"x": big(f(rng, N, 128, 4 * C)), "u": np.array(f(rng, N, 128, 512)), "v": np.array(f(rng, N, 128, 512))}
def some_links(rng):
    w = rng.choice([8, 16, 32, C], (8, 1, 1))
    return (np.arange(C) + 1 + (rng.random((8, 2, C)) * w).astype(np.int64)) % C
def links_of(rng):
    return np.stack([gtable(some_links(rng).reshape(8, 2 * C)) for r in range(N)])
def layers(rng):
    return big(f(rng, N, 128, 2048)).reshape(N, 8, 16, 4, 8, 16, 4)
def weights(rng, w):
    c, p = packed(np.ascontiguousarray(w).reshape(N, 128, 2048), rng)
    return {"wc": c, "ws": p}
def setup_inputs(rng):
    return {**numbers_of(rng), "nb": links_of(rng), **weights(rng, layers(rng))}
def setup_inputs_ties(rng):
    d = numbers_of(rng)
    o = rng.permutation(N)
    k = rng.integers(-1, 3, (N, 8, C))
    k[o[1]] = rng.integers(-3, 0, (8, C))
    k[o[2]] = 1
    x = d["x"].reshape(N, 8, 16, C, 4)
    x[:, :, 0] = 0
    x[:, :, 0, :, 0] = k.astype(np.float32).astype(BF)
    u = d["u"].reshape(N, 128, 128, 4)
    u[:, :, ::16] = 0
    for h in range(0, 128, 16): u[:, h, h, 0] = 1
    u[o[0], :, ::16] = 0
    w = layers(rng)
    w[:, :, :, :, :, 0] = 0
    return {"x": x.reshape(N, 128, 4 * C), "u": u.reshape(N, 128, 512), "v": d["v"], "nb": links_of(rng), **weights(rng, w)}
def setup_inputs_near(rng):
    d = numbers_of(rng)
    x = d["x"].astype(np.float32).reshape(N, 8, 16, C, 4)
    x[:, :, 0] = 0
    x[:, :, 8:] = 0
    s = rng.integers(0, 16, (N, 8, C))
    s = ((s[:, :, :, None] >> np.arange(4)) & 1) * np.exp2(np.arange(4) - 23.0)
    u = d["u"].reshape(N, 128, 128, 4)
    u[:, :, ::16] = 0
    nb = np.stack([some_links(rng) for r in range(N)])
    n = np.arange(C)
    first = n // 3 * 3 % (C - C % 3)
    o = rng.permutation(N) % 4
    for r in range(N):
        k = 1.0 if o[r] == 0 else 2.0 ** -30
        if o[r] < 2:
            x[r, :, 0, :, 0] = rng.choice([-1.0, 1.0], (8, C))
            x[r, :, 11, :, 0] = 2.0 ** -10
            x[r, :, 8] = s[r]
            g, e = rng.integers(8), rng.permutation(C)
            nb[r, g, 0, e], nb[r, g, 1, e] = e[first + (n + 1) % 3], e[first + (n + 2) % 3]
            x[r, g, 0, C - 1, 0] = 1.0
            x[r, g, 8, C - 1] = np.exp2(np.arange(4) - 23.0)
        elif o[r] == 2:
            x[r, :, 8, :, 0] = rng.integers(-1, 3, (8, C)) * 2.0 ** -29
            for g in rng.permutation(8)[:4]: x[r, g, 8, rng.integers(C), 0] = rng.choice([-1.0, 1.0]) * 2.0 ** 29
        else:
            x[r, :, 0, :, 0] = rng.choice([0.0, 0.0, 0.0, 0.0, 0.0, 0.0, 1.0, -1.0], (8, C))
            x[r, :, 8] = s[r] * rng.choice([-1.0, 1.0], (8, C, 1))
        for h in range(0, 128, 16):
            u[r, h, h, 0] = 1.0 if o[r] == 3 else 0.0 if o[r] == 2 else k
            u[r, h + 8, h] = k
            if o[r] < 2: u[r, h + 11, h, 0] = k
    w = layers(rng)
    for i in [0, 8, 9, 10, 11, 12, 13, 14, 15]:
        w[:, :, i] = 0
        w[:, :, :, :, :, i] = 0
    return {"x": x.reshape(N, 128, 4 * C).astype(BF), "u": u.reshape(N, 128, 512), "v": d["v"], "nb": np.stack([gtable(nb[r].reshape(8, 2 * C)) for r in range(N)]), **weights(rng, w)}
def setup_inputs_huge(rng):
    d = numbers_of(rng)
    c = rng.choice([-1.0, 1.0], (N, 1, C, 1))
    c[rng.permutation(N)[:N // 2]] = -1.0
    x = 2.0 ** 30 * (0.6 + 0.2 * rng.random((N, 128, C, 4))) * c
    u = d["u"].reshape(N, 128, 128, 4)
    u[:, :, ::16] = (2.0 ** 30 * (1.0 - 0.1 * rng.random((N, 128, 8, 4)))).astype(np.float32).astype(BF)
    w = np.zeros((N, 128, 4, 128, 4), np.float32)
    i = np.arange(128)
    for b in range(4): w[:, i, b, i, b] = -2
    return {"x": x.astype(np.float32).reshape(N, 128, 4 * C).astype(BF), "u": u.reshape(N, 128, 512), "v": d["v"], "nb": links_of(rng), **weights(rng, w.astype(BF))}
def setup_inputs_forms(rng):
    d = numbers_of(rng)
    x = d["x"].astype(np.float32).reshape(N, 8, 16, C, 4)
    a = (1.0 + (2 * rng.integers(0, 64, (N, 8, 8, C, 4)) + 1) * 2.0 ** -7) * np.exp2(-rng.integers(8, 14, (N, 8, 8, C, 4)).astype(np.float64))
    x[:, :, :8] = a * rng.choice([-1.0, 1.0], a.shape)
    x[:, :, 0, :, 0] = rng.choice([1.875, 1.96875], (N, 8, C))
    x[:, :, 1, :, 0] = rng.integers(8, 10, (N, 8, C)) * rng.choice([-1.0, 1.0], (N, 8, C)) * 2.0 ** -16
    u = d["u"].reshape(N, 128, 128, 4)
    u[:, :, ::16] = 0
    for h in range(0, 128, 16): u[:, h + 1, h, 0] = 1
    nb = np.stack([some_links(rng) for r in range(N)])
    o = rng.permutation(N) % 4
    for r in range(N):
        count = rng.permutation([M, M, M, M - 1, M + 1, 1, 0, C])
        for g in range(8):
            if o[r] == 0: nb[r, g, 1] = nb[r, g, 0]
            if o[r] in (1, 2):
                n = rng.integers(0, 2 * L - 1, C)
                n[:2 * L - 2] = np.arange(1, 2 * L - 1)
                n[2 * L - 2] = 2 * L - 2
                if o[r] == 1: n[L - 2] = 2 * L - 2
                else: n[2 * L - 3] = 0
                m = n.copy()
                e = 2 * L - 1 + np.arange(min(int(count[g]), C - 2 * L + 1))
                if o[r] == 1: n[e] = rng.integers(0, 2, len(e)) * (L - 1)
                else: n[e] = rng.integers(0, 2 * L - 2, len(e))
                m[e] = (n[e] + L - 1) % (2 * L - 2)
                k = rng.permutation(C)
                nb[r, g, 0, k], nb[r, g, 1, k] = k[n], k[m]
    return {"x": x.reshape(N, 128, 4 * C).astype(BF), "u": u.reshape(N, 128, 512), "v": d["v"], "nb": np.stack([gtable(nb[r].reshape(8, 2 * C)) for r in range(N)]), **weights(rng, layers(rng))}
def setup_inputs_spread(rng):
    d = setup_inputs(rng)
    d["x"] = big(wide(rng, N, 128, 4 * C, cols=6))
    return d
def check_inputs(d):
    b = []
    for k in ("x", "u", "v"):
        a = np.abs(d[k].astype(np.float32))
        if not (np.isfinite(a).all() and ((a == 0) | (a >= 2.0 ** -30) & (a <= 2.0 ** 30)).all()): b.append("a value of " + k)
    if not ((d["nb"] >= 0) & (d["nb"] < C)).all(): b.append("an entry of nb")
    none, least, most = [emit(mx_ref.quantize(np.full((128, 16), k, np.float32).astype(BF)))[1][0, 0] for k in (0.0, 2.0 ** -30, 2.0 ** 30)]
    for r in range(N):
        if ((d["wc"][r] == 0x7F) | (d["wc"][r] == 0xFF)).any(): b.append("wc: a code that is no number")
        s = mx_ref.live(d["ws"][r])
        if ((s != none) & ((s < least) | (s > most))).any(): b.append("ws: a scale out of range")
    return b
def bubbles(a, s):
    at = lambda t, e: np.take_along_axis(t, e, axis=1)
    c = np.where(s > 0, a[:, C:], a[:, :C])
    p, q = [a[:, :C]], [a[:, C:]]
    for k in range(1, L):
        p.append(at(c, p[-1]))
        q.append(at(c, q[-1]))
    i, j = np.full((8, C), -1), np.full((8, C), -1)
    for n in reversed(range(2 * L - 1)):
        for k in reversed(range(max(0, n - L + 1), min(n, L - 1) + 1)):
            met = p[k] == q[n - k]
            i[met], j[met] = k, n - k
    is_bubble = (i >= 0) & (p[0] != q[0])
    o = np.lexsort((-s, ~is_bubble))[:, :M]
    filled = at(is_bubble, o)
    g, k = np.arange(8)[:, None, None], np.arange(L)
    np0 = np.stack(p, axis=2)[g, o[:, :, None], np.minimum(k, at(i, o)[:, :, None])]
    nq0 = np.stack(q, axis=2)[g, o[:, :, None], np.minimum(k, at(j, o)[:, :, None])]
    one = at(s, at(q[0], o)) > at(s, at(p[0], o))
    new = a.copy()
    h, m = np.nonzero(filled)
    new[h, (o + C * ~one)[h, m]] = np0[h, m, L - 1]
    slots = [np.where(filled[:, :, None], t, -1).reshape(8, L * M) for t in (np0, nq0, np.where(one[:, :, None], nq0, np0))]
    e = np.full((8, C), -1)
    for n in reversed(range(L * M)):
        h = np.flatnonzero(slots[2][:, n] >= 0)
        e[h, slots[2][h, n]] = n
    return slots[0], slots[1], e, new
def reference(x, u, v, nb, wc, ws):
    qu = [mx_ref.quantize(u[r]) for r in range(N)]
    lay = [pk(wc[r], ws[r]) for r in range(N)]
    now = [x[r] for r in range(N)]
    links = [gentries(nb[r]).astype(np.int64) for r in range(N)]
    for t in range(R):
        own, sent, place = [], [], []
        for r in range(N):
            q = mx_ref.quantize(now[r])
            own.append(decode(q))
            s = mx_ref.matmul(qu[r], q)[::16] + np.float32(0.0)
            a, b, e, links[r] = bubbles(links[r], s)
            place.append(e)
            w = own[r].astype(BF)
            sent.append(mx_ref.quantize(((gcols(w, a).astype(np.float32) + gcols(w, b).astype(np.float32)) * np.float32(0.5)).astype(BF)))
        for r in range(N):
            came, made = sent[(r - 1) % N], []
            for b in range(4):
                h = mx_ref.matmul(pick(lay[r], np.arange(128 * b, 128 * b + 128)), came) * np.float32(0.03125)
                made.append(gpick(np.concatenate([h, np.zeros((128, 1), np.float32)], axis=1), place[r]) + own[r][:, b::4])
            now[r] = tile(made)
    y, ol = np.zeros((N, 128, C), np.float32), np.zeros((N, 8, 2 * C), np.float32)
    oc, osc = np.zeros((N, 128, 4 * C), np.uint8), np.zeros((N, 16, C), np.uint8)
    for r in range(N):
        q = mx_ref.quantize(now[r])
        y[r] = mx_ref.matmul(mx_ref.quantize(v[r]), q)
        ol[r] = links[r]
        oc[r], osc[r] = emit(q)
    return {"y": y, "ol": ol, "oc": oc, "osc": osc}

@@ -1,0 +1,473 @@
+from concourse.mybir import dt, AluOpType, AxisListType, ActivationFunctionType
+
+C, L, M, R = 288, 4, 56, 3
+NS = L * M
+BIG = 4194304.0
+EMPTY = 288.0 * 513
+
+_BUFS = """xt:1152:b xq:288:c xs:288:p ut:512:b uq:128:c us:128:p urq:384:c urs:384:p vt:512:b vq:128:c vs:128:p wq:512:c wp:512:p
+jt:528:b eq:512:c es:512:p rt:512:b rq:128:c rs:128:p fq:1440:c fs:1440:p zt:896:b fh:1216:b ff:1152:b ga:896:b hs:960 yo:288
+pf:5 mk:8 ion:304:i j16:288:i iof:304 ioo:288 ioe:288 mask16:288 tri:32:b mask4:64 tabk:304 ci:306 cj:306 sm0:128:i
+iot:18 bk:16 be:18 ul:24:o bcl:36:o li:36:i ll:36:o lf:36 lr:576 lp:352 lm:288 lt:256 lk:18:i lo:576:i lof:576 lpi:288:i
+cf:64 cl:18:o ordf:8 ordl:4:o abg:128 abi:64:i abl:32:o bn:96:i bnl:16:o t3m:128 t3g:64 ks:224 ea:4032 em:36 el:18:o
+tsb:288 sm:288 tr:256 s4:288 w1:288 w2:288 w3:288 p01:576 pr:576 tpq:576 ne:306 ij:612 bub:18:b abt0:144 ab5:144 pk:96 q3:800 p3:24
+bc:576 bc3:288 nt:288 abt:352 t3t:352 key:288 ak:1152 sg0:1152:b sg1:1152:b sg2:1152:b sg3:1152:b sg4:1152:b"""
+for _t in range(R):
+    _BUFS += " zq%d:224:c zs%d:224:p hq%d:224:c hs_%d:224:p yq%d:224:c ys%d:224:p" % ((_t,) * 6)
+_DT = {"b": "bfloat16", "c": "float8_e4m3fn_x4", "p": "uint8", "i": "int32", "o": "uint16", "f": "float32"}
+SCRATCH = {}
+for _b in _BUFS.split():
+    _p = _b.split(":") + ["f"]
+    SCRATCH[_p[0]] = ("sbuf", [128, int(_p[1])], _DT[_p[2]])
+BANKS = ["bs", "br0", "br1", "bk0", "bf0", "bf1", "bf2", "bf3"]
+for _b in BANKS:
+    SCRATCH[_b] = ("psum", [128, 512], "float32")
+SEMAPHORES = ["qv", "qs", "qt", "qg", "left", "dx", "du", "dn", "dw", "dp", "dv", "done"] + [p + str(t) for p in ("gotq", "gots", "relq", "rels") for t in range(R)]
+
+PAIRS = sorted([(i, j) for i in range(L) for j in range(L) if i + j], key=lambda e: (e[0] + e[1], e[0]))[::-1]
+
+CYC, PICK, WAKE, TRIP, LOAD = 1.0e-3, 1.5e-3, 0.07, 6.0, 2.2
+
+
+def _relays(core, dst, topo):
+    rel = [c for c in topo.cores_of(core) if c != core and topo.may_write(c, dst) and topo.die(c) == topo.die(core)]
+    return [rel[0], rel[1 % len(rel)]]
+
+
+def _piece(T, kind, k, t):
+    if k == 0:
+        return T["%sq%d" % (kind, t)][:, 0:NS].bitcast(dt.uint8)
+    return T[("hs_%d" if kind == "h" else kind + "s%d") % t][:, 0:NS]
+
+
+def _relay_program(g, core, T, topo):
+    n = 0
+    for r in range(len(T.cores)):
+        src, dst = T.cores[r], T.cores[(r + 1) % len(T.cores)]
+        if topo.may_write(src, dst):
+            continue
+        rel = _relays(src, dst, topo)
+        for t in range(R):
+            for k in range(2):
+                if rel[k] == core:
+                    rid, pid = topo.addr(dst, core)
+                    g.wait_ge(T.sem["rel" + "qs"[k] + str(t)], len(topo.engines(src, core)))
+                    g.remote_dma(_piece(T, "y", k, t), _piece(T, "h", k, t), T.sem["got" + "qs"[k] + str(t)], T.sem.left, pid, rid, topo.mask(core, dst))
+                    n += len(topo.engines(core, dst))
+    if n:
+        g.wait_ge(T.sem.left, n)
+
+
+def _order(nodes):
+    users = [[] for n in nodes]
+    for i, n in enumerate(nodes):
+        for d in n["deps"]:
+            users[d].append(i)
+    tail = [0.0] * len(nodes)
+    for i in reversed(range(len(nodes))):
+        tail[i] = nodes[i]["occ"] + nodes[i]["lat"] + max([tail[u] + WAKE for u in users[i]] + [0.0])
+    left = [len(n["deps"]) for n in nodes]
+    ready_at = [0.0] * len(nodes)
+    free, ready, out = {}, {}, []
+    for i, n in enumerate(nodes):
+        if not left[i]:
+            ready.setdefault(n["q"], []).append(i)
+    while any(ready.values()):
+        best = None
+        for q, c in ready.items():
+            if c:
+                at = [max(free.get(q, 0.0), ready_at[i]) for i in c]
+                start = min(at)
+                if best is None or start < best[0]:
+                    near = [i for i, a in zip(c, at) if a <= start + 0.02]
+                    best = (start, q, max(near, key=lambda i: tail[i]))
+        start, q, i = best
+        start = max(start, ready_at[i])
+        ready[q].remove(i)
+        out.append(i)
+        free[q] = start + nodes[i]["occ"]
+        for u in users[i]:
+            ready_at[u] = max(ready_at[u], free[q] + nodes[i]["lat"] + WAKE)
+            left[u] -= 1
+            if not left[u]:
+                ready.setdefault(nodes[u]["q"], []).append(u)
+    return out
+
+
+def rank_program(g, core, T, topo):
+    rank = T.rank_of(core)
+    if rank is None:
+        _relay_program(g, core, T, topo)
+        return
+    A = AluOpType
+    F = ActivationFunctionType
+    queue = {"v": g.vector, "s": g.scalar, "t": g.tensor, "g": g, "y": g.sync}
+    qsem = {"v": "qv", "s": "qs", "t": "qt", "g": "qg"}
+    nodes, log = [], {}
+
+    def call(q, fn, rd, wr, occ=0.06, lat=0.0, sem=None, n=1):
+        i, deps = len(nodes), {}
+        for w, regs in ((0, rd), (1, wr)):
+            for name, lo, hi, st in regs:
+                for a in log.get(name, []):
+                    if a["hi"] <= lo or hi <= a["lo"] or (st > 1 and a["st"] == st and (a["lo"] - lo) % st) or a["i"] == i:
+                        continue
+                    same = a["q"] == q and a["c"]
+                    if w == 0 and not a["w"] and (same or name not in BANKS):
+                        continue
+                    deps[a["i"]] = deps.get(a["i"], False) or not (w == 1 and same and (not a["w"] or q == "t"))
+        for w, regs in ((0, rd), (1, wr)):
+            for name, lo, hi, st in regs:
+                old = log.get(name, [])
+                if w:
+                    old = [a for a in old if not (lo <= a["lo"] and a["hi"] <= hi and (st == 1 or (a["st"] == st and (a["lo"] - lo) % st == 0)))]
+                log[name] = old + [{"lo": lo, "hi": hi, "st": st, "q": q, "c": sem is None, "w": w, "i": i}]
+        nodes.append({"q": q, "fn": fn, "deps": deps, "occ": occ, "lat": lat, "sem": sem, "n": n})
+        return i
+
+    def issue():
+        count, clock, token = {}, {q: {} for q in queue}, {}
+        for i in _order(nodes):
+            e = nodes[i]
+            q = e["q"]
+            if q == "net":
+                token[i] = (e["sem"], e["n"], {})
+                continue
+            need = {}
+            for d, awaited in e["deps"].items():
+                if awaited:
+                    sem, val, seen = token[d]
+                    if sem not in need or need[sem][1] < val:
+                        need[sem] = token[d]
+            for sem, val, seen in sorted(need.values(), key=lambda k: -len(k[2])):
+                if clock[q].get(sem, 0) < val:
+                    queue[q].wait_ge(T.sem[sem], val)
+                    clock[q][sem] = val
+                    for s, n in seen.items():
+                        clock[q][s] = max(clock[q].get(s, 0), n)
+            sem = e["sem"] or qsem[q]
+            if sem == "left":
+                e["fn"]()
+            else:
+                e["fn"]().then_inc(T.sem[sem], e["n"])
+            count[sem] = count.get(sem, 0) + e["n"]
+            token[i] = (sem, count[sem], dict(clock[q]))
+        for s in count:
+            g.wait_ge(T.sem[s], count[s])
+
+    def dma(q, sem, out, in_, rd, wr):
+        call(q, lambda: queue[q].dma_start(out, in_), rd, wr, 0.06, LOAD, sem, 16)
+
+    def r(name, lo, hi, st=1):
+        return (name, lo, hi, st)
+
+    def ap(v):
+        if not isinstance(v, tuple):
+            return v
+        return T[v[0]][:, v[1]:v[2]] if v[3] == 1 else T[v[0]][:, v[1]:v[2]:v[3]]
+
+    def wide(v, per=1.0):
+        return max(64, per * len(range(v[1], v[2], v[3]))) * CYC
+
+    def cost(out, off, per):
+        return 0.05 + PICK * len(range(out[1], out[2], out[3])) if off else wide(out, per)
+
+    def side(in_, off):
+        return ap(in_) if off is None else ap(in_).indirect(ap(off))
+
+    def views(*vs):
+        return [v for v in vs if isinstance(v, tuple)]
+
+    def half(*vs):
+        return 0.5 if all(SCRATCH[v[0]][2] == "bfloat16" for v in vs) else 1.0
+
+    def copy(out, in_, off=None):
+        call("v", lambda: g.vector.tensor_copy(ap(out), side(in_, off)), views(in_, off), [out], cost(out, off, half(out, in_)))
+
+    def tt(out, a, b, op, off=None):
+        call("v", lambda: g.vector.tensor_tensor(ap(out), side(a, off), ap(b), op), views(a, b, off), [out], cost(out, off, 1.0 if a[0] in BANKS else 2.0))
+
+    def ts(out, a, s1, op0, s2=None, op1=None, off=None):
+        if op1 is None:
+            call("v", lambda: g.vector.tensor_scalar(ap(out), side(a, off), ap(s1), None, op0), views(a, s1, off), [out], cost(out, off, half(out, a)))
+        else:
+            call("v", lambda: g.vector.tensor_scalar(ap(out), side(a, off), ap(s1), ap(s2), op0, op1), views(a, s1, s2, off), [out], cost(out, off, half(out, a)))
+
+    def fill(v, c):
+        call("v", lambda: g.vector.memset(ap(v), c), [], [v], wide(v, half(v)))
+
+    def turn(out, in_):
+        call("v", lambda: g.vector.transpose(ap(out), ap(in_)), [in_], [out], wide(out))
+
+    def least(out, in_):
+        call("v", lambda: g.vector.tensor_reduce(ap(out), ap(in_), AxisListType.X, A.min), [in_], [out], wide(in_))
+
+    def scan(out, d0, d1):
+        call("v", lambda: g.vector.tensor_tensor_scan(ap(out), ap(d0), ap(d1), 0.0, A.mult, A.add), [d0, d1], [out], wide(out))
+
+    def act(out, in_, f, bias=None, scale=None, off=None):
+        kw = {}
+        if bias is not None: kw["bias"] = ap(bias)
+        if scale is not None: kw["scale"] = ap(scale)
+        call("s", lambda: g.scalar.activation(ap(out), side(in_, off), f, **kw), views(in_, bias, scale, off), [out], cost(out, off, 1.0))
+
+    def quant(qn, sn, lo, hi, in_):
+        call("v", lambda: g.vector.quantize_mx(T[qn][:, lo:hi], T[sn][:, lo:hi], ap(in_)), [in_], [r(qn, lo, hi), r(sn, lo, hi)], 0.012 + 0.00106 * (hi - lo))
+
+    def mm(bank, n, st, sts, slo, mv, mvs, mlo, start=True, stop=True):
+        call("t", lambda: g.tensor.matmul_mx(T[bank][:, 0:n], T[st][:, slo:slo + 128], T[sts][:, slo:slo + 128], T[mv][:, mlo:mlo + n], T[mvs][:, mlo:mlo + n], start, stop),
+             [r(st, slo, slo + 128), r(sts, slo, slo + 128), r(mv, mlo, mlo + n), r(mvs, mlo, mlo + n)], [r(bank, 0, 512)], (n + 16) * CYC)
+
+    def iota(out, pattern, base, cm):
+        call("g", lambda: g.iota(ap(out), pattern, base, cm), [], [out], 0.13 + 2 * wide(out))
+
+    dma("y", "du", T.ut[:, :], T.u[:, :], [], [r("ut", 0, 512)])
+    dma("s", "dx", T.xt[:, :], T.x[:, :], [], [r("xt", 0, 4 * C)])
+    dma("y", "dn", T.li[:, :], T.nb[:, :], [], [r("li", 0, 36)])
+    dma("s", "dw", T.wq[:, :].bitcast(dt.uint8), T.wc[:, :], [], [r("wq", 0, 512)])
+    dma("y", "dp", T.wp[:, :], T.ws[:, :], [], [r("wp", 0, 512)])
+    dma("y", "dv", T.vt[:, :], T.v[:, :], [], [r("vt", 0, 512)])
+
+    iota(r("sm0", 120, 121), [[0, 1]], 0, 1)
+    iota(r("sm0", 0, 8), [[16, 8]], 0, 0)
+    iota(r("sm0", 8, 16), [[32, 4], [0, 2]], 0, 0)
+    iota(r("sm0", 16, 24), [[32, 4], [0, 2]], 16, 0)
+    iota(r("ion", 0, 304), [[1, 304]], 0, 0)
+    iota(r("sm0", 24, 42), [[32, 9], [0, 2]], 0, 0)
+    iota(r("sm0", 42, 60), [[1, 18]], 0, 0)
+    iota(r("sm0", 60, 78), [[1, 18]], 24, 0)
+    iota(r("sm0", 80, 84), [[16, 4]], 0, 0)
+    iota(r("sm0", 84, 102), [[16, 18]], 0, 0)
+    copy(r("ul", 0, 24), r("sm0", 0, 24))
+    ts(r("sm0", 121, 122), r("sm0", 120, 121), 15, A.bitwise_and)
+    ts(r("sm0", 122, 123), r("sm0", 120, 121), 2, A.logical_shift_right, 3, A.bitwise_and)
+    ts(r("sm0", 123, 124), r("sm0", 120, 121), 3, A.bitwise_and)
+    ts(r("sm0", 124, 125), r("sm0", 120, 121), 31, A.bitwise_and)
+    ts(r("sm0", 125, 126), r("sm0", 120, 121), 1, A.bitwise_and)
+    copy(r("pf", 0, 5), r("sm0", 121, 126))
+    Q, QQ, ROLE, I32, ODD = [r("pf", k, k + 1) for k in range(5)]
+    ALL4, MO, ME, M01, M23, M4 = [r("mk", k, k + 1) for k in range(6)]
+    quant("uq", "us", 0, 128, r("ut", 0, 512))
+    call("v", lambda: g.vector.tensor_copy(T.urq[:, 0:384].bitcast(dt.uint32), T.uq[:, 0:128].bitcast(dt.uint32).indirect(T.ul[:, 0:24])), [r("uq", 0, 128), r("ul", 0, 24)], [r("urq", 0, 384)], 0.6)
+    call("s", lambda: g.scalar.activation(T.urs[:, 0:384], T.us[:, 0:128].indirect(T.ul[:, 0:24]), F.Copy), [r("us", 0, 128), r("ul", 0, 24)], [r("urs", 0, 384)], 0.6)
+    ts(r("j16", 0, C), r("ion", 0, C), 15, A.bitwise_and)
+    ts(r("mask16", 0, C), r("j16", 0, C), Q, A.is_equal)
+    ts(ALL4, Q, 3.5, A.is_le)
+    tt(MO, ALL4, ODD, A.mult)
+    tt(ME, ALL4, MO, A.subtract)
+    ts(M01, Q, 1.5, A.is_le)
+    tt(M23, ALL4, M01, A.subtract)
+    ts(M4, Q, 4.0, A.is_equal)
+    copy(r("iof", 0, 304), r("ion", 0, 304))
+    ts(r("ioo", 0, C), r("iof", 0, C), MO, A.mult)
+    ts(r("ioe", 0, C), r("iof", 0, C), ME, A.mult)
+    copy(r("lf", 0, 18), r("li", 0, 18))
+    tt(r("lf", 18, 36), r("li", 18, 36), r("li", 0, 18), A.subtract)
+    copy(r("ll", 0, 36), r("li", 0, 36))
+    ts(r("tri", 0, 32), r("iof", 0, 32), I32, A.is_gt, 0.5, A.subtract)
+    fill(r("ne", 0, 306), 0.0)
+    for name, w in (("ci", 0), ("cj", 1)):
+        v = [-1] + [e[w] for e in PAIRS] + [-1, 0]
+        c = [v[t] - v[t + 1] for t in range(17)]
+        usual = max(sorted(set(c)), key=c.count)
+        fill(r(name, 0, 306), float(usual))
+        for t in range(17):
+            if c[t] != usual:
+                fill(r(name, t, 306, 17), float(c[t]))
+    fill(r("jt", 0, 528), 1.0)
+    call("g", lambda: g.affine_select(T.jt[:, 0:520], T.jt[:, 0:520], [[-1, 520]], A.is_equal, 0.0, 3, 4), [r("jt", 0, 520)], [r("jt", 0, 520)], 1.2)
+    for b in range(4):
+        quant("eq", "es", 128 * b, 128 * b + 128, r("jt", 3 - b, 515 - b))
+        fill(r("fh", 304 * b + C, 304 * b + 304), 0.0)
+    fill(r("rt", 0, 512), 0.0)
+    for a in range(4):
+        for h in range(2):
+            lo = 128 * a + 64 * h
+            call("v", lambda a=a, h=h, lo=lo: g.vector.memset(T.rt[32 * a:32 * a + 32, lo + h:lo + 64:2], 1024.0), [], [r("rt", lo, lo + 64)])
+    quant("rq", "rs", 0, 128, r("rt", 0, 512))
+    fill(r("sg4", 2, 4 * C, 4), 0.0)
+    fill(r("sg4", 3, 4 * C, 4), 0.0)
+    fill(r("pk", 0, 96), 0.0)
+    ts(r("iot", 0, 18), r("sm0", 24, 42), I32, A.add)
+    copy(r("bcl", 0, 18), r("sm0", 42, 60))
+    ts(r("cf", 54, 55), ROLE, 18.0, A.mult)
+    ts(r("sm0", 102, 120), r("sm0", 60, 78), r("cf", 54, 55), A.add)
+    copy(r("bcl", 18, 36), r("sm0", 102, 120))
+    ts(r("bk", 4, 8), r("sm0", 80, 84), Q, A.add)
+    ts(r("bk", 8, 12), r("bk", 4, 8), 288.0, A.add)
+    ts(r("bk", 0, 4), r("bk", 4, 8), float(M), A.is_ge, -1.0e7, A.mult)
+    ts(r("bk", 4, 8), r("bk", 4, 8), -1024.0, A.mult)
+    tt(r("bk", 0, 4), r("bk", 0, 4), r("bk", 4, 8), A.add)
+    ts(r("lo", 0, 64), r("ion", 0, 64), 3, A.bitwise_and)
+    ts(r("mask4", 0, 64), r("lo", 0, 64), QQ, A.is_equal)
+    fill(r("abt", C, 352), EMPTY)
+    fill(r("p3", 0, 24), 0.0)
+    ts(r("be", 0, 18), r("sm0", 84, 102), Q, A.add, -1024.0, A.mult)
+    ts(r("tabk", 0, 304), r("iof", 0, 304), 1024.0, A.mult)
+    fill(r("t3t", C, 352), 0.0)
+    for b in range(4):
+        fill(r("hs", 240 * b + NS, 240 * b + 240), 0.0)
+    fill(r("lp", C, 352), 0.0)
+    copy(r("lr", 0, 2 * C), r("iof", 0, 304), r("ll", 0, 36))
+    ts(r("lr", C, 2 * C), r("lr", C, 2 * C), 512.0, A.mult)
+    tt(r("lp", 0, C), r("lr", 0, C), r("lr", C, 2 * C), A.add)
+    quant("vq", "vs", 0, 128, r("vt", 0, 512))
+
+    n_of = len(T.cores)
+    dst, src = T.cores[(rank + 1) % n_of], T.cores[(rank - 1) % n_of]
+    direct = topo.may_write(core, dst)
+    hops = [dst, dst] if direct else _relays(core, dst, topo)
+    came = [src, src] if topo.may_write(src, core) else _relays(src, core, topo)
+
+    def evens(out, buf, lo, n):
+        tt(out, r(buf, lo, lo + n, 2), r(buf, lo + 1, lo + n, 2), A.add)
+
+    def squeeze(buf, tree, out):
+        evens(r(tree, 0, 144), buf, 0, 288)
+        evens(r(tree, 144, 216), tree, 0, 144)
+        evens(r(tree, 216, 252), tree, 144, 72)
+        evens(out, tree, 216, 36)
+
+    def send(k, t):
+        rid, pid = topo.addr(hops[k], core)
+        name = ("zq%d" if k == 0 else "zs%d") % t
+        i = call("g", lambda: g.remote_dma(_piece(T, "y" if direct else "h", k, t), _piece(T, "z", k, t), T.sem[("got" if direct else "rel") + "qs"[k] + str(t)], T.sem.left, pid, rid, topo.mask(core, hops[k])),
+                 [r(name, 0, NS)], [], 0.5, 0.0, "left", len(topo.engines(core, hops[k])))
+        far = call("net", None, [], [r("y" + name[1:], 0, NS)], 0.0, TRIP, "got" + "qs"[k] + str(t), len(topo.engines(came[k], core)))
+        nodes[far]["deps"][i] = True
+
+    for t in range(R):
+        quant("xq", "xs", 0, C, r("xt", 0, 4 * C))
+        mm("bs", C, "urq", "urs", 0, "xq", "xs", 0)
+        mm("br0", C, "urq", "urs", 128, "xq", "xs", 0)
+        mm("br1", C, "urq", "urs", 256, "xq", "xs", 0)
+        for b in range(4):
+            mm("bf%d" % b, C, "eq", "es", 128 * b, "xq", "xs", 0)
+            act(r("fh", 304 * b, 304 * b + C), r("bf%d" % b, 0, C), F.Copy, None, 0.5)
+            act(r("ff", C * b, C * b + C), r("bf%d" % b, 0, C), F.Copy)
+        turn(r("tsb", 0, C), r("bs", 0, C))
+        tt(r("sm", 0, C), r("bs", 0, C), r("mask16", 0, C), A.mult)
+        act(r("s4", 0, C), r("bs", 0, C), F.Copy, None, M4)
+        for s in range(18):
+            act(r("sg%d" % (s // 4), s % 4, 4 * C, 4), r("br%d" % (s % 2), 0, C), F.Sign, r("tsb", 16 * s, 16 * s + 1), -1.0)
+        for s in range(18):
+            lo = 128 * (s // 2) + s % 4
+            v = r("sg%d" % (s // 4), lo, min(lo + 128, 4 * C), 4)
+            tt(v, v, r("tri", 0, 32), A.add)
+        squeeze("sm", "tr", r("cf", 0, 18))
+        ts(r("cf", 18, 36), r("cf", 0, 18), 0.0, A.is_gt)
+        tt(r("cf", 18, 36), r("cf", 18, 36), r("lf", 18, 36), A.mult)
+        tt(r("cf", 36, 54), r("cf", 18, 36), r("lf", 0, 18), A.add)
+        copy(r("cl", 0, 18), r("cf", 36, 54))
+        CL = r("cl", 0, 18)
+        tt(r("w1", 0, C), r("ioo", 0, C), r("ioe", 0, C), A.add, CL)
+        ts(r("w2", 0, C), r("w1", 0, C), M23, A.mult, off=CL)
+        act(r("p01", 0, 2 * C), r("w1", 0, C), F.Copy, None, M01, r("ll", 0, 36))
+        tt(r("w3", 0, C), r("w2", 0, C), r("s4", 0, C), A.add, CL)
+        tt(r("pr", 0, 2 * C), r("w3", 0, C), r("p01", 0, 2 * C), A.add, r("ll", 0, 36))
+        turn(r("tpq", 0, 2 * C), r("pr", 0, 2 * C))
+        for k, (i, j) in enumerate(PAIRS + [(0, 0)]):
+            tt(r("ne", k + 1, 306, 17), r("tpq", i, C, 16), r("tpq", C + j, 2 * C, 16), A.not_equal)
+        scan(r("ij", 0, 306), r("ne", 0, 306), r("ci", 0, 306))
+        scan(r("ij", 306, 612), r("ne", 0, 306), r("cj", 0, 306))
+        I, IJ = r("ij", 16, 306, 17), r("ij", 16, 612, 17)
+        ts(r("bub", 0, 18), I, 0.0, A.is_ge)
+        ts(r("q3", 780, 798), I, 0.0, A.is_lt, BIG, A.mult)
+        tt(r("pk", 0, 18), r("q3", 780, 798), r("iot", 0, 18), A.add)
+        for k in range(5):
+            for s in range(4 * k, min(4 * k + 4, 18)):
+                for lo, hi, op in ((0, 32 * (s // 2), A.is_gt), (32 * (s // 2), C, A.is_ge)):
+                    if lo < hi:
+                        v = r("sg%d" % k, 4 * lo + s % 4, 4 * hi, 4)
+                        ts(v, v, 0.0, op, r("bub", s, s + 1), A.mult)
+            quant("fq", "fs", C * k, C * k + C, r("sg%d" % k, 0, 4 * C))
+            mm("bk0", C, "rq", "rs", 0, "fq", "fs", C * k, k == 0, k == 4)
+        PQ = [r("tpq", k, 2 * C, 16) for k in range(L)]
+        AB = [r("abt0", 36 * k, 36 * k + 36) for k in range(L)]
+        copy(AB[0], PQ[0])
+        for k in range(1, L):
+            o = 108 * k - 108
+            ts(r("q3", o, o + 36), IJ, float(k), A.is_ge)
+            tt(r("q3", o + 36, o + 72), PQ[k], AB[k - 1], A.subtract)
+            tt(r("q3", o + 72, o + 108), r("q3", o + 36, o + 72), r("q3", o, o + 36), A.mult)
+            tt(AB[k], AB[k - 1], r("q3", o + 72, o + 108), A.add)
+        ts(r("ab5", 0, 144), r("abt0", 0, 144), 512.0, A.mult)
+        for k in range(L):
+            tt(r("pk", 24 + 18 * k, 42 + 18 * k), r("ab5", 36 * k + 18, 36 * k + 36), r("abt0", 36 * k, 36 * k + 18), A.add)
+        act(r("bc", 0, 2 * C), r("pk", 0, 96), F.Copy, off=r("bcl", 0, 36))
+        turn(r("nt", 0, C), r("bc", 0, C))
+        turn(r("abt", 0, C), r("bc", C, 2 * C))
+        tt(r("key", 0, C), r("bk0", 0, C), r("nt", 0, C), A.add)
+        for c in range(4):
+            act(r("ak", C * c, C * c + C), r("key", 0, C), F.Abs, r("bk", c, c + 1))
+            least(r("ordf", c, c + 1), r("ak", C * c, C * c + C))
+        tt(r("ordf", 4, 8), r("ordf", 0, 4), r("bk", 8, 12), A.min)
+        copy(r("ordl", 0, 4), r("ordf", 4, 8))
+        ORD = r("ordl", 0, 4)
+        tt(r("abg", 0, 64), r("abt", 0, 352), r("mask4", 0, 64), A.mult, ORD)
+        evens(r("abg", 64, 96), "abg", 0, 64)
+        evens(r("abi", 0, 16), "abg", 64, 32)
+        ts(r("abi", 16, 32), r("abi", 0, 16), 511, A.bitwise_and)
+        ts(r("abi", 32, 48), r("abi", 0, 16), 9, A.logical_shift_right)
+        copy(r("abl", 0, 32), r("abi", 16, 48))
+        for b in range(4):
+            act(r("ga", NS * b, NS * b + NS), r("fh", 304 * b, 304 * b + 304), F.Copy, off=r("abl", 0, 14))
+            tt(r("zt", b, 4 * NS, 4), r("fh", 304 * b, 304 * b + 304), r("ga", NS * b, NS * b + NS), A.add, r("abl", 16, 30))
+        quant("zq%d" % t, "zs%d" % t, 0, NS, r("zt", 0, 4 * NS))
+        for k in range(2):
+            send(k, t)
+        o = 324
+        tt(r("q3", o, o + 36), AB[3], PQ[0], A.subtract)
+        ts(r("q3", o + 36, o + 54), r("q3", o + 18, o + 36), 512.0, A.mult)
+        tt(r("q3", o + 54, o + 72), r("q3", o, o + 18), r("q3", o + 36, o + 54), A.subtract)
+        tt(r("q3", o + 72, o + 90), r("tpq", C + 4, 2 * C, 16), r("tpq", 4, C, 16), A.is_gt)
+        tt(r("q3", o + 90, o + 108), r("q3", o + 72, o + 90), r("q3", o + 54, o + 72), A.mult)
+        tt(r("q3", o + 108, o + 126), r("ab5", 108, 126), r("tpq", 0, C, 16), A.add)
+        tt(r("q3", o + 126, o + 144), r("q3", o + 108, o + 126), r("q3", o + 90, o + 108), A.add)
+        ts(r("q3", o + 144, o + 162), r("q3", o + 72, o + 90), 262144.0, A.mult)
+        tt(r("p3", 0, 18), r("q3", o + 126, o + 144), r("q3", o + 144, o + 162), A.add)
+        act(r("bc3", 0, C), r("p3", 0, 24), F.Copy, off=r("bcl", 0, 18))
+        turn(r("t3t", 0, C), r("bc3", 0, C))
+        copy(r("t3g", 0, 64), r("t3t", 0, 352), ORD)
+        tt(r("t3m", 0, 64), r("t3t", 0, 352), r("mask4", 0, 64), A.mult, ORD)
+        evens(r("t3m", 64, 96), "t3m", 0, 64)
+        evens(r("bn", 0, 16), "t3m", 64, 32)
+        ts(r("bn", 16, 32), r("bn", 0, 16), 18, A.logical_shift_right)
+        tt(r("bn", 32, 48), r("abi", 32, 48), r("abi", 16, 32), A.subtract)
+        tt(r("bn", 48, 64), r("bn", 32, 48), r("bn", 16, 32), A.mult)
+        tt(r("bn", 64, 80), r("bn", 48, 64), r("abi", 16, 32), A.add)
+        copy(r("bnl", 0, 16), r("bn", 64, 80))
+        tt(r("ks", 0, NS), r("tabk", 0, 304), r("iof", 0, NS), A.add, r("bnl", 0, 14))
+        for k in range(18):
+            act(r("ea", NS * k, NS * k + NS), r("ks", 0, NS), F.Abs, r("be", k, k + 1))
+            least(r("em", k, k + 1), r("ea", NS * k, NS * k + NS))
+        ts(r("em", 18, 36), r("em", 0, 18), float(NS), A.min)
+        copy(r("el", 0, 18), r("em", 18, 36))
+        call("v", lambda: g.vector.tensor_copy(T.lp[:, 0:352].indirect(T.ordl[:, 0:4]), T.t3g[:, 0:64]), [r("t3g", 0, 64), ORD], [r("lp", 0, 352)], 0.25)
+        if t < R - 1:
+            tt(r("lm", 0, C), r("lp", 0, C), r("mask16", 0, C), A.mult)
+            squeeze("lm", "lt", r("lk", 0, 18))
+            ts(r("li", 0, 18), r("lk", 0, 18), 511, A.bitwise_and)
+            ts(r("li", 18, 36), r("lk", 0, 18), 9, A.logical_shift_right, 511, A.bitwise_and)
+            copy(r("ll", 0, 36), r("li", 0, 36))
+            copy(r("lf", 0, 18), r("li", 0, 18))
+            tt(r("lf", 18, 36), r("li", 18, 36), r("li", 0, 18), A.subtract)
+        else:
+            copy(r("lpi", 0, C), r("lp", 0, C))
+            ts(r("lo", 0, C), r("lpi", 0, C), 511, A.bitwise_and)
+            ts(r("lo", C, 2 * C), r("lpi", 0, C), 9, A.logical_shift_right, 511, A.bitwise_and)
+            copy(r("lof", 0, 2 * C), r("lo", 0, 2 * C))
+            dma("y", "done", T.ol[:, :], T.lof[0:128:16, :], [r("lof", 0, 2 * C)], [])
+        for b in range(4):
+            mm(BANKS[b], NS, "wq", "wp", 128 * b, "yq%d" % t, "ys%d" % t, 0)
+            act(r("hs", 240 * b, 240 * b + NS), r(BANKS[b], 0, NS), F.Copy, None, 0.03125)
+            tt(r("xt", b, 4 * C, 4), r("hs", 240 * b, 240 * b + 240), r("ff", C * b, C * b + C), A.add, r("el", 0, 18))
+
+    quant("xq", "xs", 0, C, r("xt", 0, 4 * C))
+    mm("bs", C, "vq", "vs", 0, "xq", "xs", 0)
+    act(r("yo", 0, C), r("bs", 0, C), F.Copy)
+    dma("y", "done", T.oc[:, :], T.xq[:, 0:C].bitcast(dt.uint8), [r("xq", 0, C)], [])
+    for k in range(4):
+        dma("ys"[k % 2], "done", T.osc[4 * k:4 * k + 4, :], T.xs[32 * k:32 * k + 4, 0:C], [r("xs", 0, C)], [])
+    dma("s", "done", T.y[:, :], T.yo[:, :], [r("yo", 0, C)], [])
+    issue()

@@ -3,17 +3,18 @@ from concourse.mybir import dt, AluOpType, AxisListType, ActivationFunctionType
 C, L, M, R = 288, 4, 56, 3
 NS = L * M
 BIG = 4194304.0
-EMPTY = 288.0 * 513
+EMPTY = 288 * 513
+TINY = 2.0 ** -119
 
-_BUFS = """xt:1152:b xq:288:c xs:288:p ut:512:b uq:128:c us:128:p urq:384:c urs:384:p vt:512:b vq:128:c vs:128:p wq:512:c wp:512:p
+_BUFS = """xt:1152:b ut:512:b uq:128:c us:128:p urq:384:c urs:384:p vt:512:b vq:128:c vs:128:p wq:512:c wp:512:p
 jt:528:b eq:512:c es:512:p rt:512:b rq:128:c rs:128:p fq:1440:c fs:1440:p zt:896:b fh:1216:b ff:1152:b ga:896:b hs:960 yo:288
-pf:5 mk:8 ion:304:i j16:288:i iof:304 ioo:288 ioe:288 mask16:288 tri:32:b mask4:64 tabk:304 ci:306 cj:306 sm0:128:i
-iot:18 bk:16 be:18 ul:24:o bcl:36:o li:36:i ll:36:o lf:36 lr:576 lp:352 lm:288 lt:256 lk:18:i lo:576:i lof:576 lpi:288:i
-cf:64 cl:18:o ordf:8 ordl:4:o abg:128 abi:64:i abl:32:o bn:96:i bnl:16:o t3m:128 t3g:64 ks:224 ea:4032 em:36 el:18:o
-tsb:288 sm:288 tr:256 s4:288 w1:288 w2:288 w3:288 p01:576 pr:576 tpq:576 ne:306 ij:612 bub:18:b abt0:144 ab5:144 pk:96 q3:800 p3:24
-bc:576 bc3:288 nt:288 abt:352 t3t:352 key:288 ak:1152 sg0:1152:b sg1:1152:b sg2:1152:b sg3:1152:b sg4:1152:b"""
+pf:16 ion:304:i j16:288:i iof:304 ioo:288 ioe:288 mask16:352 tri:32:b mask4:64 tabk:304 ci:306 cj:306 sm0:128:i zq:224:c zs:224:p
+iot:18 bk:16 be:18 ul:24:o bcl:36:o li:36:i ll:36:o lf:36 lpk:24 lp:352 lk:18:i lof:576
+cf:64 cl:18:o ordf:8 ordl:4:o abg:128 abi:64:i bn:96:i bnl:16:o t3m:256 ks:224 ea:4032 em:36 el:18:o
+tsb:288 sm:544 ww:1152 pp:1728 ne:306 ij:612 bub:18:b bubf:18 abt0:144 ab5:144 pk:96 q3:800
+p3:24 bc:864 nt:576 abt:352 t3t:352 ak:1152 sg0:1152:b sg1:1152:b sg2:1152:b sg3:1152:b sg4:1152:b xq3:288:c xs3:288:p"""
 for _t in range(R):
-    _BUFS += " zq%d:224:c zs%d:224:p hq%d:224:c hs_%d:224:p yq%d:224:c ys%d:224:p" % ((_t,) * 6)
+    _BUFS += " xq%d:288:c xs%d:288:p al%d:32:o hq%d:288:c hs_%d:288:p hsl%d:32:o yq%d:288:c ys%d:288:p ysl%d:32:o" % ((_t,) * 9)
 _DT = {"b": "bfloat16", "c": "float8_e4m3fn_x4", "p": "uint8", "i": "int32", "o": "uint16", "f": "float32"}
 SCRATCH = {}
 for _b in _BUFS.split():
@@ -22,22 +23,28 @@ for _b in _BUFS.split():
 BANKS = ["bs", "br0", "br1", "bk0", "bf0", "bf1", "bf2", "bf3"]
 for _b in BANKS:
     SCRATCH[_b] = ("psum", [128, 512], "float32")
-SEMAPHORES = ["qv", "qs", "qt", "qg", "left", "dx", "du", "dn", "dw", "dp", "dv", "done"] + [p + str(t) for p in ("gotq", "gots", "relq", "rels") for t in range(R)]
+PART = {"tr": ("sm", 288), "s4": ("ww", 0), "w1": ("ww", 288), "w2": ("ww", 576), "w3": ("ww", 864), "p01": ("pp", 0), "pr": ("pp", 576),
+        "tpq": ("pp", 1152), "bc3": ("bc", 576), "key": ("nt", 288), "t3g": ("t3m", 128), "t3q": ("t3m", 192), "mk": ("pf", 8)}
+SEMAPHORES = ["qv", "qs", "qt", "qg", "left", "dx", "du", "dn", "dw", "dp", "dv", "done"] + [p + k + str(t) for p in ("got", "rel") for k in "qsl" for t in range(R)]
 
+SHARE = 2
+VE = (2, 6, 10, 14)
 PAIRS = sorted([(i, j) for i in range(L) for j in range(L) if i + j], key=lambda e: (e[0] + e[1], e[0]))[::-1]
 
-CYC, PICK, WAKE, TRIP, LOAD = 1.0e-3, 1.5e-3, 0.07, 6.0, 2.2
+CYC, PICK, ACT, WAKE, TRIP, LOAD = 1.0e-3, 1.5e-3, 0.02, 0.2, (8.0, 8.0, 5.0), 2.2
 
 
 def _relays(core, dst, topo):
     rel = [c for c in topo.cores_of(core) if c != core and topo.may_write(c, dst) and topo.die(c) == topo.die(core)]
-    return [rel[0], rel[1 % len(rel)]]
+    return [rel[0], rel[1 % len(rel)], rel[1 % len(rel)]]
 
 
 def _piece(T, kind, k, t):
     if k == 0:
-        return T["%sq%d" % (kind, t)][:, 0:NS].bitcast(dt.uint8)
-    return T[("hs_%d" if kind == "h" else kind + "s%d") % t][:, 0:NS]
+        return T["%sq%d" % (kind, t)][:, 0:C].bitcast(dt.uint8)
+    if k == 1:
+        return T[("hs_%d" if kind == "h" else kind + "s%d") % t][:, 0:C]
+    return T[{"x": "al%d", "h": "hsl%d", "y": "ysl%d"}[kind] % t][:, 0:32]
 
 
 def _relay_program(g, core, T, topo):
@@ -48,11 +55,11 @@ def _relay_program(g, core, T, topo):
             continue
         rel = _relays(src, dst, topo)
         for t in range(R):
-            for k in range(2):
+            for k in range(3):
                 if rel[k] == core:
                     rid, pid = topo.addr(dst, core)
-                    g.wait_ge(T.sem["rel" + "qs"[k] + str(t)], len(topo.engines(src, core)))
-                    g.remote_dma(_piece(T, "y", k, t), _piece(T, "h", k, t), T.sem["got" + "qs"[k] + str(t)], T.sem.left, pid, rid, topo.mask(core, dst))
+                    g.wait_ge(T.sem["rel" + "qsl"[k] + str(t)], len(topo.engines(src, core)))
+                    g.remote_dma(_piece(T, "y", k, t), _piece(T, "h", k, t), T.sem["got" + "qsl"[k] + str(t)], T.sem.left, pid, rid, topo.mask(core, dst))
                     n += len(topo.engines(core, dst))
     if n:
         g.wait_ge(T.sem.left, n)
@@ -159,7 +166,8 @@ def rank_program(g, core, T, topo):
         call(q, lambda: queue[q].dma_start(out, in_), rd, wr, 0.06, LOAD, sem, 16)
 
     def r(name, lo, hi, st=1):
-        return (name, lo, hi, st)
+        name, o = PART.get(name, (name, 0))
+        return (name, lo + o, hi + o, st)
 
     def ap(v):
         if not isinstance(v, tuple):
@@ -196,11 +204,20 @@ def rank_program(g, core, T, topo):
     def fill(v, c):
         call("v", lambda: g.vector.memset(ap(v), c), [], [v], wide(v, half(v)))
 
+    def gfill(v, c):
+        giota(v, [[0, len(range(v[1], v[2], v[3]))]], c)
+
+    def giota(v, pattern, base):
+        call("g", lambda: g.iota(ap(v), pattern, base, 0, allow_small_or_imprecise_dtypes=True), [], [v], 0.13 + 2 * wide(v))
+
+    def iota(out, pattern, base, cm):
+        call("g", lambda: g.iota(ap(out), pattern, base, cm), [], [out], 0.13 + 2 * wide(out))
+
     def turn(out, in_):
         call("v", lambda: g.vector.transpose(ap(out), ap(in_)), [in_], [out], wide(out))
 
     def least(out, in_):
-        call("v", lambda: g.vector.tensor_reduce(ap(out), ap(in_), AxisListType.X, A.min), [in_], [out], wide(in_))
+        call("v", lambda: g.vector.tensor_reduce(ap(out), ap(in_), AxisListType.X, A.min, apply_absolute_value=True), [in_], [out], wide(in_))
 
     def scan(out, d0, d1):
         call("v", lambda: g.vector.tensor_tensor_scan(ap(out), ap(d0), ap(d1), 0.0, A.mult, A.add), [d0, d1], [out], wide(out))
@@ -209,7 +226,7 @@ def rank_program(g, core, T, topo):
         kw = {}
         if bias is not None: kw["bias"] = ap(bias)
         if scale is not None: kw["scale"] = ap(scale)
-        call("s", lambda: g.scalar.activation(ap(out), side(in_, off), f, **kw), views(in_, bias, scale, off), [out], cost(out, off, 1.0))
+        call("s", lambda: g.scalar.activation(ap(out), side(in_, off), f, **kw), views(in_, bias, scale, off), [out], cost(out, off, 1.0) + (0.0 if off else ACT))
 
     def quant(qn, sn, lo, hi, in_):
         call("v", lambda: g.vector.quantize_mx(T[qn][:, lo:hi], T[sn][:, lo:hi], ap(in_)), [in_], [r(qn, lo, hi), r(sn, lo, hi)], 0.012 + 0.00106 * (hi - lo))
@@ -217,9 +234,6 @@ def rank_program(g, core, T, topo):
     def mm(bank, n, st, sts, slo, mv, mvs, mlo, start=True, stop=True):
         call("t", lambda: g.tensor.matmul_mx(T[bank][:, 0:n], T[st][:, slo:slo + 128], T[sts][:, slo:slo + 128], T[mv][:, mlo:mlo + n], T[mvs][:, mlo:mlo + n], start, stop),
              [r(st, slo, slo + 128), r(sts, slo, slo + 128), r(mv, mlo, mlo + n), r(mvs, mlo, mlo + n)], [r(bank, 0, 512)], (n + 16) * CYC)
-
-    def iota(out, pattern, base, cm):
-        call("g", lambda: g.iota(ap(out), pattern, base, cm), [], [out], 0.13 + 2 * wide(out))
 
     dma("y", "du", T.ut[:, :], T.u[:, :], [], [r("ut", 0, 512)])
     dma("s", "dx", T.xt[:, :], T.x[:, :], [], [r("xt", 0, 4 * C)])
@@ -233,6 +247,7 @@ def rank_program(g, core, T, topo):
     iota(r("sm0", 8, 16), [[32, 4], [0, 2]], 0, 0)
     iota(r("sm0", 16, 24), [[32, 4], [0, 2]], 16, 0)
     iota(r("ion", 0, 304), [[1, 304]], 0, 0)
+    giota(r("iof", 0, 304), [[1, 304]], 0)
     iota(r("sm0", 24, 42), [[32, 9], [0, 2]], 0, 0)
     iota(r("sm0", 42, 60), [[1, 18]], 0, 0)
     iota(r("sm0", 60, 78), [[1, 18]], 24, 0)
@@ -258,13 +273,13 @@ def rank_program(g, core, T, topo):
     ts(M01, Q, 1.5, A.is_le)
     tt(M23, ALL4, M01, A.subtract)
     ts(M4, Q, 4.0, A.is_equal)
-    copy(r("iof", 0, 304), r("ion", 0, 304))
-    ts(r("ioo", 0, C), r("iof", 0, C), MO, A.mult)
-    ts(r("ioe", 0, C), r("iof", 0, C), ME, A.mult)
+    act(r("ioo", 0, C), r("iof", 0, C), F.Copy, None, MO)
+    act(r("ioe", 0, C), r("iof", 0, C), F.Copy, None, ME)
     copy(r("lf", 0, 18), r("li", 0, 18))
     tt(r("lf", 18, 36), r("li", 18, 36), r("li", 0, 18), A.subtract)
     copy(r("ll", 0, 36), r("li", 0, 36))
     ts(r("tri", 0, 32), r("iof", 0, 32), I32, A.is_gt, 0.5, A.subtract)
+    ts(r("tri", 0, 32), r("tri", 0, 32), TINY, A.mult)
     fill(r("ne", 0, 306), 0.0)
     for name, w in (("ci", 0), ("cj", 1)):
         v = [-1] + [e[w] for e in PAIRS] + [-1, 0]
@@ -274,20 +289,20 @@ def rank_program(g, core, T, topo):
         for t in range(17):
             if c[t] != usual:
                 fill(r(name, t, 306, 17), float(c[t]))
-    fill(r("jt", 0, 528), 1.0)
+    gfill(r("jt", 0, 528), 1)
     call("g", lambda: g.affine_select(T.jt[:, 0:520], T.jt[:, 0:520], [[-1, 520]], A.is_equal, 0.0, 3, 4), [r("jt", 0, 520)], [r("jt", 0, 520)], 1.2)
     for b in range(4):
         quant("eq", "es", 128 * b, 128 * b + 128, r("jt", 3 - b, 515 - b))
-        fill(r("fh", 304 * b + C, 304 * b + 304), 0.0)
-    fill(r("rt", 0, 512), 0.0)
+        gfill(r("fh", 304 * b + C, 304 * b + 304), 0)
+    gfill(r("rt", 0, 512), 0)
     for a in range(4):
         for h in range(2):
             lo = 128 * a + 64 * h
-            call("v", lambda a=a, h=h, lo=lo: g.vector.memset(T.rt[32 * a:32 * a + 32, lo + h:lo + 64:2], 1024.0), [], [r("rt", lo, lo + 64)])
+            call("s", lambda v=T.rt[32 * a:32 * a + 32, lo + h:lo + 64:2]: g.scalar.activation(v, v, F.Identity, bias=1024.0), [r("rt", lo, lo + 64)], [r("rt", lo, lo + 64)])
     quant("rq", "rs", 0, 128, r("rt", 0, 512))
-    fill(r("sg4", 2, 4 * C, 4), 0.0)
-    fill(r("sg4", 3, 4 * C, 4), 0.0)
-    fill(r("pk", 0, 96), 0.0)
+    gfill(r("sg4", 2, 4 * C, 4), 0)
+    gfill(r("sg4", 3, 4 * C, 4), 0)
+    gfill(r("pk", 0, 96), 0)
     ts(r("iot", 0, 18), r("sm0", 24, 42), I32, A.add)
     copy(r("bcl", 0, 18), r("sm0", 42, 60))
     ts(r("cf", 54, 55), ROLE, 18.0, A.mult)
@@ -298,52 +313,56 @@ def rank_program(g, core, T, topo):
     ts(r("bk", 0, 4), r("bk", 4, 8), float(M), A.is_ge, -1.0e7, A.mult)
     ts(r("bk", 4, 8), r("bk", 4, 8), -1024.0, A.mult)
     tt(r("bk", 0, 4), r("bk", 0, 4), r("bk", 4, 8), A.add)
-    ts(r("lo", 0, 64), r("ion", 0, 64), 3, A.bitwise_and)
-    ts(r("mask4", 0, 64), r("lo", 0, 64), QQ, A.is_equal)
-    fill(r("abt", C, 352), EMPTY)
-    fill(r("p3", 0, 24), 0.0)
+    ts(r("abi", 0, 64), r("ion", 0, 64), 3, A.bitwise_and)
+    ts(r("mask4", 0, 64), r("abi", 0, 64), QQ, A.is_equal)
+    gfill(r("abt", C, 352), EMPTY)
+    gfill(r("p3", 0, 24), 0)
     ts(r("be", 0, 18), r("sm0", 84, 102), Q, A.add, -1024.0, A.mult)
-    ts(r("tabk", 0, 304), r("iof", 0, 304), 1024.0, A.mult)
-    fill(r("t3t", C, 352), 0.0)
+    act(r("tabk", 0, 304), r("iof", 0, 304), F.Copy, None, 1024.0)
+    gfill(r("t3t", C, 352), 0)
     for b in range(4):
-        fill(r("hs", 240 * b + NS, 240 * b + 240), 0.0)
-    fill(r("lp", C, 352), 0.0)
-    copy(r("lr", 0, 2 * C), r("iof", 0, 304), r("ll", 0, 36))
-    ts(r("lr", C, 2 * C), r("lr", C, 2 * C), 512.0, A.mult)
-    tt(r("lp", 0, C), r("lr", 0, C), r("lr", C, 2 * C), A.add)
+        gfill(r("hs", 240 * b + NS, 240 * b + 240), 0)
+    gfill(r("lp", C, 352), 0)
+    gfill(r("mask16", C, 352), 0)
+    gfill(r("lpk", 18, 24), 0)
+    ts(r("cf", 0, 18), r("li", 18, 36), 512.0, A.mult)
+    tt(r("lpk", 0, 18), r("cf", 0, 18), r("li", 0, 18), A.add)
+    tt(r("lp", 0, C), r("lpk", 0, 24), r("mask16", 0, C), A.mult, r("bcl", 0, 18))
     quant("vq", "vs", 0, 128, r("vt", 0, 512))
 
     n_of = len(T.cores)
     dst, src = T.cores[(rank + 1) % n_of], T.cores[(rank - 1) % n_of]
     direct = topo.may_write(core, dst)
-    hops = [dst, dst] if direct else _relays(core, dst, topo)
-    came = [src, src] if topo.may_write(src, core) else _relays(src, core, topo)
+    hops = [dst] * 3 if direct else _relays(core, dst, topo)
+    came = [src] * 3 if topo.may_write(src, core) else _relays(src, core, topo)
 
     def evens(out, buf, lo, n):
         tt(out, r(buf, lo, lo + n, 2), r(buf, lo + 1, lo + n, 2), A.add)
 
-    def squeeze(buf, tree, out):
-        evens(r(tree, 0, 144), buf, 0, 288)
-        evens(r(tree, 144, 216), tree, 0, 144)
-        evens(r(tree, 216, 252), tree, 144, 72)
-        evens(out, tree, 216, 36)
+    def squeeze(buf, out):
+        evens(r("tr", 0, 144), buf, 0, 288)
+        evens(r("tr", 144, 216), "tr", 0, 144)
+        evens(r("tr", 216, 252), "tr", 144, 72)
+        evens(out, "tr", 216, 36)
 
     def send(k, t):
         rid, pid = topo.addr(hops[k], core)
-        name = ("zq%d" if k == 0 else "zs%d") % t
-        i = call("g", lambda: g.remote_dma(_piece(T, "y" if direct else "h", k, t), _piece(T, "z", k, t), T.sem[("got" if direct else "rel") + "qs"[k] + str(t)], T.sem.left, pid, rid, topo.mask(core, hops[k])),
-                 [r(name, 0, NS)], [], 0.5, 0.0, "left", len(topo.engines(core, hops[k])))
-        far = call("net", None, [], [r("y" + name[1:], 0, NS)], 0.0, TRIP, "got" + "qs"[k] + str(t), len(topo.engines(came[k], core)))
+        name, n = (("xq%d", C), ("xs%d", C), ("al%d", 32))[k]
+        i = call("g", lambda: g.remote_dma(_piece(T, "y" if direct else "h", k, t), _piece(T, "x", k, t), T.sem[("got" if direct else "rel") + "qsl"[k] + str(t)], T.sem.left, pid, rid, topo.mask(core, hops[k])),
+                 [r(name % t, 0, n)], [], 0.5, 0.0, "left", len(topo.engines(core, hops[k])))
+        far = call("net", None, [], [r(("yq%d", "ys%d", "ysl%d")[k] % t, 0, n)], 0.0, TRIP[k], "got" + "qsl"[k] + str(t), len(topo.engines(came[k], core)))
         nodes[far]["deps"][i] = True
 
     for t in range(R):
-        quant("xq", "xs", 0, C, r("xt", 0, 4 * C))
-        mm("bs", C, "urq", "urs", 0, "xq", "xs", 0)
-        mm("br0", C, "urq", "urs", 128, "xq", "xs", 0)
-        mm("br1", C, "urq", "urs", 256, "xq", "xs", 0)
+        XQ, XS = "xq%d" % t, "xs%d" % t
+        quant(XQ, XS, 0, C, r("xt", 0, 4 * C))
+        for k in range(2):
+            send(k, t)
+        mm("bs", C, "urq", "urs", 0, XQ, XS, 0)
+        mm("br0", C, "urq", "urs", 128, XQ, XS, 0)
+        mm("br1", C, "urq", "urs", 256, XQ, XS, 0)
         for b in range(4):
-            mm("bf%d" % b, C, "eq", "es", 128 * b, "xq", "xs", 0)
-            act(r("fh", 304 * b, 304 * b + C), r("bf%d" % b, 0, C), F.Copy, None, 0.5)
+            mm("bf%d" % b, C, "eq", "es", 128 * b, XQ, XS, 0)
             act(r("ff", C * b, C * b + C), r("bf%d" % b, 0, C), F.Copy)
         turn(r("tsb", 0, C), r("bs", 0, C))
         tt(r("sm", 0, C), r("bs", 0, C), r("mask16", 0, C), A.mult)
@@ -354,7 +373,7 @@ def rank_program(g, core, T, topo):
             lo = 128 * (s // 2) + s % 4
             v = r("sg%d" % (s // 4), lo, min(lo + 128, 4 * C), 4)
             tt(v, v, r("tri", 0, 32), A.add)
-        squeeze("sm", "tr", r("cf", 0, 18))
+        squeeze("sm", r("cf", 0, 18))
         ts(r("cf", 18, 36), r("cf", 0, 18), 0.0, A.is_gt)
         tt(r("cf", 18, 36), r("cf", 18, 36), r("lf", 18, 36), A.mult)
         tt(r("cf", 36, 54), r("cf", 18, 36), r("lf", 0, 18), A.add)
@@ -372,6 +391,7 @@ def rank_program(g, core, T, topo):
         scan(r("ij", 306, 612), r("ne", 0, 306), r("cj", 0, 306))
         I, IJ = r("ij", 16, 306, 17), r("ij", 16, 612, 17)
         ts(r("bub", 0, 18), I, 0.0, A.is_ge)
+        ts(r("bubf", 0, 18), I, 0.0, A.is_ge)
         ts(r("q3", 780, 798), I, 0.0, A.is_lt, BIG, A.mult)
         tt(r("pk", 0, 18), r("q3", 780, 798), r("iot", 0, 18), A.add)
         for k in range(5):
@@ -379,7 +399,10 @@ def rank_program(g, core, T, topo):
                 for lo, hi, op in ((0, 32 * (s // 2), A.is_gt), (32 * (s // 2), C, A.is_ge)):
                     if lo < hi:
                         v = r("sg%d" % k, 4 * lo + s % 4, 4 * hi, 4)
-                        ts(v, v, 0.0, op, r("bub", s, s + 1), A.mult)
+                        if lo == 0 and s // 2 >= SHARE:
+                            act(v, v, F.Relu, None, r("bubf", s, s + 1))
+                        else:
+                            ts(v, v, 0.0, op, r("bub", s, s + 1), A.mult)
             quant("fq", "fs", C * k, C * k + C, r("sg%d" % k, 0, 4 * C))
             mm("bk0", C, "rq", "rs", 0, "fq", "fs", C * k, k == 0, k == 4)
         PQ = [r("tpq", k, 2 * C, 16) for k in range(L)]
@@ -409,13 +432,8 @@ def rank_program(g, core, T, topo):
         evens(r("abi", 0, 16), "abg", 64, 32)
         ts(r("abi", 16, 32), r("abi", 0, 16), 511, A.bitwise_and)
         ts(r("abi", 32, 48), r("abi", 0, 16), 9, A.logical_shift_right)
-        copy(r("abl", 0, 32), r("abi", 16, 48))
-        for b in range(4):
-            act(r("ga", NS * b, NS * b + NS), r("fh", 304 * b, 304 * b + 304), F.Copy, off=r("abl", 0, 14))
-            tt(r("zt", b, 4 * NS, 4), r("fh", 304 * b, 304 * b + 304), r("ga", NS * b, NS * b + NS), A.add, r("abl", 16, 30))
-        quant("zq%d" % t, "zs%d" % t, 0, NS, r("zt", 0, 4 * NS))
-        for k in range(2):
-            send(k, t)
+        copy(r("al%d" % t, 0, 32), r("abi", 16, 48))
+        send(2, t)
         o = 324
         tt(r("q3", o, o + 36), AB[3], PQ[0], A.subtract)
         ts(r("q3", o + 36, o + 54), r("q3", o + 18, o + 36), 512.0, A.mult)
@@ -439,35 +457,44 @@ def rank_program(g, core, T, topo):
         copy(r("bnl", 0, 16), r("bn", 64, 80))
         tt(r("ks", 0, NS), r("tabk", 0, 304), r("iof", 0, NS), A.add, r("bnl", 0, 14))
         for k in range(18):
-            act(r("ea", NS * k, NS * k + NS), r("ks", 0, NS), F.Abs, r("be", k, k + 1))
+            if k in VE:
+                ts(r("ea", NS * k, NS * k + NS), r("ks", 0, NS), r("be", k, k + 1), A.add)
+            else:
+                act(r("ea", NS * k, NS * k + NS), r("ks", 0, NS), F.Abs, r("be", k, k + 1))
             least(r("em", k, k + 1), r("ea", NS * k, NS * k + NS))
         ts(r("em", 18, 36), r("em", 0, 18), float(NS), A.min)
         copy(r("el", 0, 18), r("em", 18, 36))
-        call("v", lambda: g.vector.tensor_copy(T.lp[:, 0:352].indirect(T.ordl[:, 0:4]), T.t3g[:, 0:64]), [r("t3g", 0, 64), ORD], [r("lp", 0, 352)], 0.25)
+        tt(r("t3q", 0, 64), r("mask16", 0, 352), r("t3g", 0, 64), A.mult, ORD)
+        W = r("t3q", 0, 64)
+        call("v", lambda W=W: g.vector.tensor_copy(T.lp[:, 0:352].indirect(T.ordl[:, 0:4]), ap(W)), [W, ORD], [r("lp", 0, 352)], 0.25)
+        squeeze("lp", r("lk", 0, 18))
+        ts(r("li", 0, 18), r("lk", 0, 18), 511, A.bitwise_and)
+        ts(r("li", 18, 36), r("lk", 0, 18), 9, A.logical_shift_right, 511, A.bitwise_and)
+        copy(r("ll", 0, 36), r("li", 0, 36))
         if t < R - 1:
-            tt(r("lm", 0, C), r("lp", 0, C), r("mask16", 0, C), A.mult)
-            squeeze("lm", "lt", r("lk", 0, 18))
-            ts(r("li", 0, 18), r("lk", 0, 18), 511, A.bitwise_and)
-            ts(r("li", 18, 36), r("lk", 0, 18), 9, A.logical_shift_right, 511, A.bitwise_and)
-            copy(r("ll", 0, 36), r("li", 0, 36))
             copy(r("lf", 0, 18), r("li", 0, 18))
             tt(r("lf", 18, 36), r("li", 18, 36), r("li", 0, 18), A.subtract)
         else:
-            copy(r("lpi", 0, C), r("lp", 0, C))
-            ts(r("lo", 0, C), r("lpi", 0, C), 511, A.bitwise_and)
-            ts(r("lo", C, 2 * C), r("lpi", 0, C), 9, A.logical_shift_right, 511, A.bitwise_and)
-            copy(r("lof", 0, 2 * C), r("lo", 0, 2 * C))
+            act(r("lof", 0, 2 * C), r("iof", 0, 304), F.Copy, off=r("ll", 0, 36))
             dma("y", "done", T.ol[:, :], T.lof[0:128:16, :], [r("lof", 0, 2 * C)], [])
         for b in range(4):
-            mm(BANKS[b], NS, "wq", "wp", 128 * b, "yq%d" % t, "ys%d" % t, 0)
+            mm("bf%d" % b, C, "eq", "es", 128 * b, "yq%d" % t, "ys%d" % t, 0)
+            act(r("fh", 304 * b, 304 * b + C), r("bf%d" % b, 0, C), F.Copy, None, 0.5)
+        for b in range(4):
+            H = r("fh", 304 * b, 304 * b + 304)
+            act(r("ga", NS * b, NS * b + NS), H, F.Copy, off=r("ysl%d" % t, 0, 14))
+            tt(r("zt", b, 4 * NS, 4), H, r("ga", NS * b, NS * b + NS), A.add, r("ysl%d" % t, 16, 30))
+        quant("zq", "zs", 0, NS, r("zt", 0, 4 * NS))
+        for b in range(4):
+            mm(BANKS[b], NS, "wq", "wp", 128 * b, "zq", "zs", 0)
             act(r("hs", 240 * b, 240 * b + NS), r(BANKS[b], 0, NS), F.Copy, None, 0.03125)
             tt(r("xt", b, 4 * C, 4), r("hs", 240 * b, 240 * b + 240), r("ff", C * b, C * b + C), A.add, r("el", 0, 18))
 
-    quant("xq", "xs", 0, C, r("xt", 0, 4 * C))
-    mm("bs", C, "vq", "vs", 0, "xq", "xs", 0)
+    quant("xq3", "xs3", 0, C, r("xt", 0, 4 * C))
+    mm("bs", C, "vq", "vs", 0, "xq3", "xs3", 0)
     act(r("yo", 0, C), r("bs", 0, C), F.Copy)
-    dma("y", "done", T.oc[:, :], T.xq[:, 0:C].bitcast(dt.uint8), [r("xq", 0, C)], [])
+    dma("y", "done", T.oc[:, :], T.xq3[:, 0:C].bitcast(dt.uint8), [r("xq3", 0, C)], [])
     for k in range(4):
-        dma("ys"[k % 2], "done", T.osc[4 * k:4 * k + 4, :], T.xs[32 * k:32 * k + 4, 0:C], [r("xs", 0, C)], [])
+        dma("ys"[k % 2], "done", T.osc[4 * k:4 * k + 4, :], T.xs3[32 * k:32 * k + 4, 0:C], [r("xs3", 0, C)], [])
     dma("s", "done", T.y[:, :], T.yo[:, :], [r("yo", 0, C)], [])
     issue()

from concourse.mybir import dt, AluOpType, AxisListType, ActivationFunctionType

C, L, M, R = 288, 4, 56, 3
NS = L * M
BIG = 4194304.0
EMPTY = 288 * 513
TINY = 2.0 ** -119

_BUFS = """xt:1152:b ut:512:b uq:128:c us:128:p urq:384:c urs:384:p vt:512:b vq:128:c vs:128:p wq:512:c wp:512:p
jt:528:b eq:512:c es:512:p rt:512:b rq:128:c rs:128:p fq:1440:c fs:1440:p zt:896:b fh:1216:b ff:1152:b ga:896:b hs:960 yo:288
pf:16 ion:304:i j16:288:i iof:304 ioo:288 ioe:288 mask16:352 tri:32:b mask4:64 tabk:304 ci:306 cj:306 sm0:128:i zq:224:c zs:224:p
iot:18 bk:16 be:18 ul:24:o bcl:36:o li:36:i ll:36:o lf:36 lpk:24 lp:352 lk:18:i lof:576
cf:64 cl:18:o ordf:8 ordl:4:o abg:128 abi:64:i bn:96:i bnl:16:o t3m:256 ks:224 ea:4032 em:36 el:18:o
tsb:288 sm:544 ww:1152 pp:1728 ne:306 ij:612 bub:18:b bubf:18 abt0:144 ab5:144 pk:96 q3:800
p3:24 bc:864 nt:576 abt:352 t3t:352 ak:1152 sg0:1152:b sg1:1152:b sg2:1152:b sg3:1152:b sg4:1152:b xq3:288:c xs3:288:p"""
for _t in range(R):
    _BUFS += " xq%d:288:c xs%d:288:p al%d:32:o hq%d:288:c hs_%d:288:p hsl%d:32:o yq%d:288:c ys%d:288:p ysl%d:32:o" % ((_t,) * 9)
_DT = {"b": "bfloat16", "c": "float8_e4m3fn_x4", "p": "uint8", "i": "int32", "o": "uint16", "f": "float32"}
SCRATCH = {}
for _b in _BUFS.split():
    _p = _b.split(":") + ["f"]
    SCRATCH[_p[0]] = ("sbuf", [128, int(_p[1])], _DT[_p[2]])
BANKS = ["bs", "br0", "br1", "bk0", "bf0", "bf1", "bf2", "bf3"]
for _b in BANKS:
    SCRATCH[_b] = ("psum", [128, 512], "float32")
PART = {"tr": ("sm", 288), "s4": ("ww", 0), "w1": ("ww", 288), "w2": ("ww", 576), "w3": ("ww", 864), "p01": ("pp", 0), "pr": ("pp", 576),
        "tpq": ("pp", 1152), "bc3": ("bc", 576), "key": ("nt", 288), "t3g": ("t3m", 128), "t3q": ("t3m", 192), "mk": ("pf", 8)}
SEMAPHORES = ["qv", "qs", "qt", "qg", "left", "dx", "du", "dn", "dw", "dp", "dv", "done"] + [p + k + str(t) for p in ("got", "rel") for k in "qsl" for t in range(R)]

SHARE = 2
VE = (2, 6, 10, 14)
PAIRS = sorted([(i, j) for i in range(L) for j in range(L) if i + j], key=lambda e: (e[0] + e[1], e[0]))[::-1]

CYC, PICK, ACT, WAKE, TRIP, LOAD = 1.0e-3, 1.5e-3, 0.02, 0.2, (8.0, 8.0, 5.0), 2.2


def _relays(core, dst, topo):
    rel = [c for c in topo.cores_of(core) if c != core and topo.may_write(c, dst) and topo.die(c) == topo.die(core)]
    return [rel[0], rel[1 % len(rel)], rel[1 % len(rel)]]


def _piece(T, kind, k, t):
    if k == 0:
        return T["%sq%d" % (kind, t)][:, 0:C].bitcast(dt.uint8)
    if k == 1:
        return T[("hs_%d" if kind == "h" else kind + "s%d") % t][:, 0:C]
    return T[{"x": "al%d", "h": "hsl%d", "y": "ysl%d"}[kind] % t][:, 0:32]


def _relay_program(g, core, T, topo):
    n = 0
    for r in range(len(T.cores)):
        src, dst = T.cores[r], T.cores[(r + 1) % len(T.cores)]
        if topo.may_write(src, dst):
            continue
        rel = _relays(src, dst, topo)
        for t in range(R):
            for k in range(3):
                if rel[k] == core:
                    rid, pid = topo.addr(dst, core)
                    g.wait_ge(T.sem["rel" + "qsl"[k] + str(t)], len(topo.engines(src, core)))
                    g.remote_dma(_piece(T, "y", k, t), _piece(T, "h", k, t), T.sem["got" + "qsl"[k] + str(t)], T.sem.left, pid, rid, topo.mask(core, dst))
                    n += len(topo.engines(core, dst))
    if n:
        g.wait_ge(T.sem.left, n)


def _order(nodes):
    users = [[] for n in nodes]
    for i, n in enumerate(nodes):
        for d in n["deps"]:
            users[d].append(i)
    tail = [0.0] * len(nodes)
    for i in reversed(range(len(nodes))):
        tail[i] = nodes[i]["occ"] + nodes[i]["lat"] + max([tail[u] + WAKE for u in users[i]] + [0.0])
    left = [len(n["deps"]) for n in nodes]
    ready_at = [0.0] * len(nodes)
    free, ready, out = {}, {}, []
    for i, n in enumerate(nodes):
        if not left[i]:
            ready.setdefault(n["q"], []).append(i)
    while any(ready.values()):
        best = None
        for q, c in ready.items():
            if c:
                at = [max(free.get(q, 0.0), ready_at[i]) for i in c]
                start = min(at)
                if best is None or start < best[0]:
                    near = [i for i, a in zip(c, at) if a <= start + 0.02]
                    best = (start, q, max(near, key=lambda i: tail[i]))
        start, q, i = best
        start = max(start, ready_at[i])
        ready[q].remove(i)
        out.append(i)
        free[q] = start + nodes[i]["occ"]
        for u in users[i]:
            ready_at[u] = max(ready_at[u], free[q] + nodes[i]["lat"] + WAKE)
            left[u] -= 1
            if not left[u]:
                ready.setdefault(nodes[u]["q"], []).append(u)
    return out


def rank_program(g, core, T, topo):
    rank = T.rank_of(core)
    if rank is None:
        _relay_program(g, core, T, topo)
        return
    A = AluOpType
    F = ActivationFunctionType
    queue = {"v": g.vector, "s": g.scalar, "t": g.tensor, "g": g, "y": g.sync}
    qsem = {"v": "qv", "s": "qs", "t": "qt", "g": "qg"}
    nodes, log = [], {}

    def call(q, fn, rd, wr, occ=0.06, lat=0.0, sem=None, n=1):
        i, deps = len(nodes), {}
        for w, regs in ((0, rd), (1, wr)):
            for name, lo, hi, st in regs:
                for a in log.get(name, []):
                    if a["hi"] <= lo or hi <= a["lo"] or (st > 1 and a["st"] == st and (a["lo"] - lo) % st) or a["i"] == i:
                        continue
                    same = a["q"] == q and a["c"]
                    if w == 0 and not a["w"] and (same or name not in BANKS):
                        continue
                    deps[a["i"]] = deps.get(a["i"], False) or not (w == 1 and same and (not a["w"] or q == "t"))
        for w, regs in ((0, rd), (1, wr)):
            for name, lo, hi, st in regs:
                old = log.get(name, [])
                if w:
                    old = [a for a in old if not (lo <= a["lo"] and a["hi"] <= hi and (st == 1 or (a["st"] == st and (a["lo"] - lo) % st == 0)))]
                log[name] = old + [{"lo": lo, "hi": hi, "st": st, "q": q, "c": sem is None, "w": w, "i": i}]
        nodes.append({"q": q, "fn": fn, "deps": deps, "occ": occ, "lat": lat, "sem": sem, "n": n})
        return i

    def issue():
        count, clock, token = {}, {q: {} for q in queue}, {}
        for i in _order(nodes):
            e = nodes[i]
            q = e["q"]
            if q == "net":
                token[i] = (e["sem"], e["n"], {})
                continue
            need = {}
            for d, awaited in e["deps"].items():
                if awaited:
                    sem, val, seen = token[d]
                    if sem not in need or need[sem][1] < val:
                        need[sem] = token[d]
            for sem, val, seen in sorted(need.values(), key=lambda k: -len(k[2])):
                if clock[q].get(sem, 0) < val:
                    queue[q].wait_ge(T.sem[sem], val)
                    clock[q][sem] = val
                    for s, n in seen.items():
                        clock[q][s] = max(clock[q].get(s, 0), n)
            sem = e["sem"] or qsem[q]
            if sem == "left":
                e["fn"]()
            else:
                e["fn"]().then_inc(T.sem[sem], e["n"])
            count[sem] = count.get(sem, 0) + e["n"]
            token[i] = (sem, count[sem], dict(clock[q]))
        for s in count:
            g.wait_ge(T.sem[s], count[s])

    def dma(q, sem, out, in_, rd, wr):
        call(q, lambda: queue[q].dma_start(out, in_), rd, wr, 0.06, LOAD, sem, 16)

    def r(name, lo, hi, st=1):
        name, o = PART.get(name, (name, 0))
        return (name, lo + o, hi + o, st)

    def ap(v):
        if not isinstance(v, tuple):
            return v
        return T[v[0]][:, v[1]:v[2]] if v[3] == 1 else T[v[0]][:, v[1]:v[2]:v[3]]

    def wide(v, per=1.0):
        return max(64, per * len(range(v[1], v[2], v[3]))) * CYC

    def cost(out, off, per):
        return 0.05 + PICK * len(range(out[1], out[2], out[3])) if off else wide(out, per)

    def side(in_, off):
        return ap(in_) if off is None else ap(in_).indirect(ap(off))

    def views(*vs):
        return [v for v in vs if isinstance(v, tuple)]

    def half(*vs):
        return 0.5 if all(SCRATCH[v[0]][2] == "bfloat16" for v in vs) else 1.0

    def copy(out, in_, off=None):
        call("v", lambda: g.vector.tensor_copy(ap(out), side(in_, off)), views(in_, off), [out], cost(out, off, half(out, in_)))

    def tt(out, a, b, op, off=None):
        call("v", lambda: g.vector.tensor_tensor(ap(out), side(a, off), ap(b), op), views(a, b, off), [out], cost(out, off, 1.0 if a[0] in BANKS else 2.0))

    def ts(out, a, s1, op0, s2=None, op1=None, off=None):
        if op1 is None:
            call("v", lambda: g.vector.tensor_scalar(ap(out), side(a, off), ap(s1), None, op0), views(a, s1, off), [out], cost(out, off, half(out, a)))
        else:
            call("v", lambda: g.vector.tensor_scalar(ap(out), side(a, off), ap(s1), ap(s2), op0, op1), views(a, s1, s2, off), [out], cost(out, off, half(out, a)))

    def fill(v, c):
        call("v", lambda: g.vector.memset(ap(v), c), [], [v], wide(v, half(v)))

    def gfill(v, c):
        giota(v, [[0, len(range(v[1], v[2], v[3]))]], c)

    def giota(v, pattern, base):
        call("g", lambda: g.iota(ap(v), pattern, base, 0, allow_small_or_imprecise_dtypes=True), [], [v], 0.13 + 2 * wide(v))

    def iota(out, pattern, base, cm):
        call("g", lambda: g.iota(ap(out), pattern, base, cm), [], [out], 0.13 + 2 * wide(out))

    def turn(out, in_):
        call("v", lambda: g.vector.transpose(ap(out), ap(in_)), [in_], [out], wide(out))

    def least(out, in_):
        call("v", lambda: g.vector.tensor_reduce(ap(out), ap(in_), AxisListType.X, A.min, apply_absolute_value=True), [in_], [out], wide(in_))

    def scan(out, d0, d1):
        call("v", lambda: g.vector.tensor_tensor_scan(ap(out), ap(d0), ap(d1), 0.0, A.mult, A.add), [d0, d1], [out], wide(out))

    def act(out, in_, f, bias=None, scale=None, off=None):
        kw = {}
        if bias is not None: kw["bias"] = ap(bias)
        if scale is not None: kw["scale"] = ap(scale)
        call("s", lambda: g.scalar.activation(ap(out), side(in_, off), f, **kw), views(in_, bias, scale, off), [out], cost(out, off, 1.0) + (0.0 if off else ACT))

    def quant(qn, sn, lo, hi, in_):
        call("v", lambda: g.vector.quantize_mx(T[qn][:, lo:hi], T[sn][:, lo:hi], ap(in_)), [in_], [r(qn, lo, hi), r(sn, lo, hi)], 0.012 + 0.00106 * (hi - lo))

    def mm(bank, n, st, sts, slo, mv, mvs, mlo, start=True, stop=True):
        call("t", lambda: g.tensor.matmul_mx(T[bank][:, 0:n], T[st][:, slo:slo + 128], T[sts][:, slo:slo + 128], T[mv][:, mlo:mlo + n], T[mvs][:, mlo:mlo + n], start, stop),
             [r(st, slo, slo + 128), r(sts, slo, slo + 128), r(mv, mlo, mlo + n), r(mvs, mlo, mlo + n)], [r(bank, 0, 512)], (n + 16) * CYC)

    dma("y", "du", T.ut[:, :], T.u[:, :], [], [r("ut", 0, 512)])
    dma("s", "dx", T.xt[:, :], T.x[:, :], [], [r("xt", 0, 4 * C)])
    dma("y", "dn", T.li[:, :], T.nb[:, :], [], [r("li", 0, 36)])
    dma("s", "dw", T.wq[:, :].bitcast(dt.uint8), T.wc[:, :], [], [r("wq", 0, 512)])
    dma("y", "dp", T.wp[:, :], T.ws[:, :], [], [r("wp", 0, 512)])
    dma("y", "dv", T.vt[:, :], T.v[:, :], [], [r("vt", 0, 512)])

    iota(r("sm0", 120, 121), [[0, 1]], 0, 1)
    iota(r("sm0", 0, 8), [[16, 8]], 0, 0)
    iota(r("sm0", 8, 16), [[32, 4], [0, 2]], 0, 0)
    iota(r("sm0", 16, 24), [[32, 4], [0, 2]], 16, 0)
    iota(r("ion", 0, 304), [[1, 304]], 0, 0)
    giota(r("iof", 0, 304), [[1, 304]], 0)
    iota(r("sm0", 24, 42), [[32, 9], [0, 2]], 0, 0)
    iota(r("sm0", 42, 60), [[1, 18]], 0, 0)
    iota(r("sm0", 60, 78), [[1, 18]], 24, 0)
    iota(r("sm0", 80, 84), [[16, 4]], 0, 0)
    iota(r("sm0", 84, 102), [[16, 18]], 0, 0)
    copy(r("ul", 0, 24), r("sm0", 0, 24))
    ts(r("sm0", 121, 122), r("sm0", 120, 121), 15, A.bitwise_and)
    ts(r("sm0", 122, 123), r("sm0", 120, 121), 2, A.logical_shift_right, 3, A.bitwise_and)
    ts(r("sm0", 123, 124), r("sm0", 120, 121), 3, A.bitwise_and)
    ts(r("sm0", 124, 125), r("sm0", 120, 121), 31, A.bitwise_and)
    ts(r("sm0", 125, 126), r("sm0", 120, 121), 1, A.bitwise_and)
    copy(r("pf", 0, 5), r("sm0", 121, 126))
    Q, QQ, ROLE, I32, ODD = [r("pf", k, k + 1) for k in range(5)]
    ALL4, MO, ME, M01, M23, M4 = [r("mk", k, k + 1) for k in range(6)]
    quant("uq", "us", 0, 128, r("ut", 0, 512))
    call("v", lambda: g.vector.tensor_copy(T.urq[:, 0:384].bitcast(dt.uint32), T.uq[:, 0:128].bitcast(dt.uint32).indirect(T.ul[:, 0:24])), [r("uq", 0, 128), r("ul", 0, 24)], [r("urq", 0, 384)], 0.6)
    call("s", lambda: g.scalar.activation(T.urs[:, 0:384], T.us[:, 0:128].indirect(T.ul[:, 0:24]), F.Copy), [r("us", 0, 128), r("ul", 0, 24)], [r("urs", 0, 384)], 0.6)
    ts(r("j16", 0, C), r("ion", 0, C), 15, A.bitwise_and)
    ts(r("mask16", 0, C), r("j16", 0, C), Q, A.is_equal)
    ts(ALL4, Q, 3.5, A.is_le)
    tt(MO, ALL4, ODD, A.mult)
    tt(ME, ALL4, MO, A.subtract)
    ts(M01, Q, 1.5, A.is_le)
    tt(M23, ALL4, M01, A.subtract)
    ts(M4, Q, 4.0, A.is_equal)
    act(r("ioo", 0, C), r("iof", 0, C), F.Copy, None, MO)
    act(r("ioe", 0, C), r("iof", 0, C), F.Copy, None, ME)
    copy(r("lf", 0, 18), r("li", 0, 18))
    tt(r("lf", 18, 36), r("li", 18, 36), r("li", 0, 18), A.subtract)
    copy(r("ll", 0, 36), r("li", 0, 36))
    ts(r("tri", 0, 32), r("iof", 0, 32), I32, A.is_gt, 0.5, A.subtract)
    ts(r("tri", 0, 32), r("tri", 0, 32), TINY, A.mult)
    fill(r("ne", 0, 306), 0.0)
    for name, w in (("ci", 0), ("cj", 1)):
        v = [-1] + [e[w] for e in PAIRS] + [-1, 0]
        c = [v[t] - v[t + 1] for t in range(17)]
        usual = max(sorted(set(c)), key=c.count)
        fill(r(name, 0, 306), float(usual))
        for t in range(17):
            if c[t] != usual:
                fill(r(name, t, 306, 17), float(c[t]))
    gfill(r("jt", 0, 528), 1)
    call("g", lambda: g.affine_select(T.jt[:, 0:520], T.jt[:, 0:520], [[-1, 520]], A.is_equal, 0.0, 3, 4), [r("jt", 0, 520)], [r("jt", 0, 520)], 1.2)
    for b in range(4):
        quant("eq", "es", 128 * b, 128 * b + 128, r("jt", 3 - b, 515 - b))
        gfill(r("fh", 304 * b + C, 304 * b + 304), 0)
    gfill(r("rt", 0, 512), 0)
    for a in range(4):
        for h in range(2):
            lo = 128 * a + 64 * h
            call("s", lambda v=T.rt[32 * a:32 * a + 32, lo + h:lo + 64:2]: g.scalar.activation(v, v, F.Identity, bias=1024.0), [r("rt", lo, lo + 64)], [r("rt", lo, lo + 64)])
    quant("rq", "rs", 0, 128, r("rt", 0, 512))
    gfill(r("sg4", 2, 4 * C, 4), 0)
    gfill(r("sg4", 3, 4 * C, 4), 0)
    gfill(r("pk", 0, 96), 0)
    ts(r("iot", 0, 18), r("sm0", 24, 42), I32, A.add)
    copy(r("bcl", 0, 18), r("sm0", 42, 60))
    ts(r("cf", 54, 55), ROLE, 18.0, A.mult)
    ts(r("sm0", 102, 120), r("sm0", 60, 78), r("cf", 54, 55), A.add)
    copy(r("bcl", 18, 36), r("sm0", 102, 120))
    ts(r("bk", 4, 8), r("sm0", 80, 84), Q, A.add)
    ts(r("bk", 8, 12), r("bk", 4, 8), 288.0, A.add)
    ts(r("bk", 0, 4), r("bk", 4, 8), float(M), A.is_ge, -1.0e7, A.mult)
    ts(r("bk", 4, 8), r("bk", 4, 8), -1024.0, A.mult)
    tt(r("bk", 0, 4), r("bk", 0, 4), r("bk", 4, 8), A.add)
    ts(r("abi", 0, 64), r("ion", 0, 64), 3, A.bitwise_and)
    ts(r("mask4", 0, 64), r("abi", 0, 64), QQ, A.is_equal)
    gfill(r("abt", C, 352), EMPTY)
    gfill(r("p3", 0, 24), 0)
    ts(r("be", 0, 18), r("sm0", 84, 102), Q, A.add, -1024.0, A.mult)
    act(r("tabk", 0, 304), r("iof", 0, 304), F.Copy, None, 1024.0)
    gfill(r("t3t", C, 352), 0)
    for b in range(4):
        gfill(r("hs", 240 * b + NS, 240 * b + 240), 0)
    gfill(r("lp", C, 352), 0)
    gfill(r("mask16", C, 352), 0)
    gfill(r("lpk", 18, 24), 0)
    ts(r("cf", 0, 18), r("li", 18, 36), 512.0, A.mult)
    tt(r("lpk", 0, 18), r("cf", 0, 18), r("li", 0, 18), A.add)
    tt(r("lp", 0, C), r("lpk", 0, 24), r("mask16", 0, C), A.mult, r("bcl", 0, 18))
    quant("vq", "vs", 0, 128, r("vt", 0, 512))

    n_of = len(T.cores)
    dst, src = T.cores[(rank + 1) % n_of], T.cores[(rank - 1) % n_of]
    direct = topo.may_write(core, dst)
    hops = [dst] * 3 if direct else _relays(core, dst, topo)
    came = [src] * 3 if topo.may_write(src, core) else _relays(src, core, topo)

    def evens(out, buf, lo, n):
        tt(out, r(buf, lo, lo + n, 2), r(buf, lo + 1, lo + n, 2), A.add)

    def squeeze(buf, out):
        evens(r("tr", 0, 144), buf, 0, 288)
        evens(r("tr", 144, 216), "tr", 0, 144)
        evens(r("tr", 216, 252), "tr", 144, 72)
        evens(out, "tr", 216, 36)

    def send(k, t):
        rid, pid = topo.addr(hops[k], core)
        name, n = (("xq%d", C), ("xs%d", C), ("al%d", 32))[k]
        i = call("g", lambda: g.remote_dma(_piece(T, "y" if direct else "h", k, t), _piece(T, "x", k, t), T.sem[("got" if direct else "rel") + "qsl"[k] + str(t)], T.sem.left, pid, rid, topo.mask(core, hops[k])),
                 [r(name % t, 0, n)], [], 0.5, 0.0, "left", len(topo.engines(core, hops[k])))
        far = call("net", None, [], [r(("yq%d", "ys%d", "ysl%d")[k] % t, 0, n)], 0.0, TRIP[k], "got" + "qsl"[k] + str(t), len(topo.engines(came[k], core)))
        nodes[far]["deps"][i] = True

    for t in range(R):
        XQ, XS = "xq%d" % t, "xs%d" % t
        quant(XQ, XS, 0, C, r("xt", 0, 4 * C))
        for k in range(2):
            send(k, t)
        mm("bs", C, "urq", "urs", 0, XQ, XS, 0)
        mm("br0", C, "urq", "urs", 128, XQ, XS, 0)
        mm("br1", C, "urq", "urs", 256, XQ, XS, 0)
        for b in range(4):
            mm("bf%d" % b, C, "eq", "es", 128 * b, XQ, XS, 0)
            act(r("ff", C * b, C * b + C), r("bf%d" % b, 0, C), F.Copy)
        turn(r("tsb", 0, C), r("bs", 0, C))
        tt(r("sm", 0, C), r("bs", 0, C), r("mask16", 0, C), A.mult)
        act(r("s4", 0, C), r("bs", 0, C), F.Copy, None, M4)
        for s in range(18):
            act(r("sg%d" % (s // 4), s % 4, 4 * C, 4), r("br%d" % (s % 2), 0, C), F.Sign, r("tsb", 16 * s, 16 * s + 1), -1.0)
        for s in range(18):
            lo = 128 * (s // 2) + s % 4
            v = r("sg%d" % (s // 4), lo, min(lo + 128, 4 * C), 4)
            tt(v, v, r("tri", 0, 32), A.add)
        squeeze("sm", r("cf", 0, 18))
        ts(r("cf", 18, 36), r("cf", 0, 18), 0.0, A.is_gt)
        tt(r("cf", 18, 36), r("cf", 18, 36), r("lf", 18, 36), A.mult)
        tt(r("cf", 36, 54), r("cf", 18, 36), r("lf", 0, 18), A.add)
        copy(r("cl", 0, 18), r("cf", 36, 54))
        CL = r("cl", 0, 18)
        tt(r("w1", 0, C), r("ioo", 0, C), r("ioe", 0, C), A.add, CL)
        ts(r("w2", 0, C), r("w1", 0, C), M23, A.mult, off=CL)
        act(r("p01", 0, 2 * C), r("w1", 0, C), F.Copy, None, M01, r("ll", 0, 36))
        tt(r("w3", 0, C), r("w2", 0, C), r("s4", 0, C), A.add, CL)
        tt(r("pr", 0, 2 * C), r("w3", 0, C), r("p01", 0, 2 * C), A.add, r("ll", 0, 36))
        turn(r("tpq", 0, 2 * C), r("pr", 0, 2 * C))
        for k, (i, j) in enumerate(PAIRS + [(0, 0)]):
            tt(r("ne", k + 1, 306, 17), r("tpq", i, C, 16), r("tpq", C + j, 2 * C, 16), A.not_equal)
        scan(r("ij", 0, 306), r("ne", 0, 306), r("ci", 0, 306))
        scan(r("ij", 306, 612), r("ne", 0, 306), r("cj", 0, 306))
        I, IJ = r("ij", 16, 306, 17), r("ij", 16, 612, 17)
        ts(r("bub", 0, 18), I, 0.0, A.is_ge)
        ts(r("bubf", 0, 18), I, 0.0, A.is_ge)
        ts(r("q3", 780, 798), I, 0.0, A.is_lt, BIG, A.mult)
        tt(r("pk", 0, 18), r("q3", 780, 798), r("iot", 0, 18), A.add)
        for k in range(5):
            for s in range(4 * k, min(4 * k + 4, 18)):
                for lo, hi, op in ((0, 32 * (s // 2), A.is_gt), (32 * (s // 2), C, A.is_ge)):
                    if lo < hi:
                        v = r("sg%d" % k, 4 * lo + s % 4, 4 * hi, 4)
                        if lo == 0 and s // 2 >= SHARE:
                            act(v, v, F.Relu, None, r("bubf", s, s + 1))
                        else:
                            ts(v, v, 0.0, op, r("bub", s, s + 1), A.mult)
            quant("fq", "fs", C * k, C * k + C, r("sg%d" % k, 0, 4 * C))
            mm("bk0", C, "rq", "rs", 0, "fq", "fs", C * k, k == 0, k == 4)
        PQ = [r("tpq", k, 2 * C, 16) for k in range(L)]
        AB = [r("abt0", 36 * k, 36 * k + 36) for k in range(L)]
        copy(AB[0], PQ[0])
        for k in range(1, L):
            o = 108 * k - 108
            ts(r("q3", o, o + 36), IJ, float(k), A.is_ge)
            tt(r("q3", o + 36, o + 72), PQ[k], AB[k - 1], A.subtract)
            tt(r("q3", o + 72, o + 108), r("q3", o + 36, o + 72), r("q3", o, o + 36), A.mult)
            tt(AB[k], AB[k - 1], r("q3", o + 72, o + 108), A.add)
        ts(r("ab5", 0, 144), r("abt0", 0, 144), 512.0, A.mult)
        for k in range(L):
            tt(r("pk", 24 + 18 * k, 42 + 18 * k), r("ab5", 36 * k + 18, 36 * k + 36), r("abt0", 36 * k, 36 * k + 18), A.add)
        act(r("bc", 0, 2 * C), r("pk", 0, 96), F.Copy, off=r("bcl", 0, 36))
        turn(r("nt", 0, C), r("bc", 0, C))
        turn(r("abt", 0, C), r("bc", C, 2 * C))
        tt(r("key", 0, C), r("bk0", 0, C), r("nt", 0, C), A.add)
        for c in range(4):
            act(r("ak", C * c, C * c + C), r("key", 0, C), F.Abs, r("bk", c, c + 1))
            least(r("ordf", c, c + 1), r("ak", C * c, C * c + C))
        tt(r("ordf", 4, 8), r("ordf", 0, 4), r("bk", 8, 12), A.min)
        copy(r("ordl", 0, 4), r("ordf", 4, 8))
        ORD = r("ordl", 0, 4)
        tt(r("abg", 0, 64), r("abt", 0, 352), r("mask4", 0, 64), A.mult, ORD)
        evens(r("abg", 64, 96), "abg", 0, 64)
        evens(r("abi", 0, 16), "abg", 64, 32)
        ts(r("abi", 16, 32), r("abi", 0, 16), 511, A.bitwise_and)
        ts(r("abi", 32, 48), r("abi", 0, 16), 9, A.logical_shift_right)
        copy(r("al%d" % t, 0, 32), r("abi", 16, 48))
        send(2, t)
        o = 324
        tt(r("q3", o, o + 36), AB[3], PQ[0], A.subtract)
        ts(r("q3", o + 36, o + 54), r("q3", o + 18, o + 36), 512.0, A.mult)
        tt(r("q3", o + 54, o + 72), r("q3", o, o + 18), r("q3", o + 36, o + 54), A.subtract)
        tt(r("q3", o + 72, o + 90), r("tpq", C + 4, 2 * C, 16), r("tpq", 4, C, 16), A.is_gt)
        tt(r("q3", o + 90, o + 108), r("q3", o + 72, o + 90), r("q3", o + 54, o + 72), A.mult)
        tt(r("q3", o + 108, o + 126), r("ab5", 108, 126), r("tpq", 0, C, 16), A.add)
        tt(r("q3", o + 126, o + 144), r("q3", o + 108, o + 126), r("q3", o + 90, o + 108), A.add)
        ts(r("q3", o + 144, o + 162), r("q3", o + 72, o + 90), 262144.0, A.mult)
        tt(r("p3", 0, 18), r("q3", o + 126, o + 144), r("q3", o + 144, o + 162), A.add)
        act(r("bc3", 0, C), r("p3", 0, 24), F.Copy, off=r("bcl", 0, 18))
        turn(r("t3t", 0, C), r("bc3", 0, C))
        copy(r("t3g", 0, 64), r("t3t", 0, 352), ORD)
        tt(r("t3m", 0, 64), r("t3t", 0, 352), r("mask4", 0, 64), A.mult, ORD)
        evens(r("t3m", 64, 96), "t3m", 0, 64)
        evens(r("bn", 0, 16), "t3m", 64, 32)
        ts(r("bn", 16, 32), r("bn", 0, 16), 18, A.logical_shift_right)
        tt(r("bn", 32, 48), r("abi", 32, 48), r("abi", 16, 32), A.subtract)
        tt(r("bn", 48, 64), r("bn", 32, 48), r("bn", 16, 32), A.mult)
        tt(r("bn", 64, 80), r("bn", 48, 64), r("abi", 16, 32), A.add)
        copy(r("bnl", 0, 16), r("bn", 64, 80))
        tt(r("ks", 0, NS), r("tabk", 0, 304), r("iof", 0, NS), A.add, r("bnl", 0, 14))
        for k in range(18):
            if k in VE:
                ts(r("ea", NS * k, NS * k + NS), r("ks", 0, NS), r("be", k, k + 1), A.add)
            else:
                act(r("ea", NS * k, NS * k + NS), r("ks", 0, NS), F.Abs, r("be", k, k + 1))
            least(r("em", k, k + 1), r("ea", NS * k, NS * k + NS))
        ts(r("em", 18, 36), r("em", 0, 18), float(NS), A.min)
        copy(r("el", 0, 18), r("em", 18, 36))
        tt(r("t3q", 0, 64), r("mask16", 0, 352), r("t3g", 0, 64), A.mult, ORD)
        W = r("t3q", 0, 64)
        call("v", lambda W=W: g.vector.tensor_copy(T.lp[:, 0:352].indirect(T.ordl[:, 0:4]), ap(W)), [W, ORD], [r("lp", 0, 352)], 0.25)
        squeeze("lp", r("lk", 0, 18))
        ts(r("li", 0, 18), r("lk", 0, 18), 511, A.bitwise_and)
        ts(r("li", 18, 36), r("lk", 0, 18), 9, A.logical_shift_right, 511, A.bitwise_and)
        copy(r("ll", 0, 36), r("li", 0, 36))
        if t < R - 1:
            copy(r("lf", 0, 18), r("li", 0, 18))
            tt(r("lf", 18, 36), r("li", 18, 36), r("li", 0, 18), A.subtract)
        else:
            act(r("lof", 0, 2 * C), r("iof", 0, 304), F.Copy, off=r("ll", 0, 36))
            dma("y", "done", T.ol[:, :], T.lof[0:128:16, :], [r("lof", 0, 2 * C)], [])
        for b in range(4):
            mm("bf%d" % b, C, "eq", "es", 128 * b, "yq%d" % t, "ys%d" % t, 0)
            act(r("fh", 304 * b, 304 * b + C), r("bf%d" % b, 0, C), F.Copy, None, 0.5)
        for b in range(4):
            H = r("fh", 304 * b, 304 * b + 304)
            act(r("ga", NS * b, NS * b + NS), H, F.Copy, off=r("ysl%d" % t, 0, 14))
            tt(r("zt", b, 4 * NS, 4), H, r("ga", NS * b, NS * b + NS), A.add, r("ysl%d" % t, 16, 30))
        quant("zq", "zs", 0, NS, r("zt", 0, 4 * NS))
        for b in range(4):
            mm(BANKS[b], NS, "wq", "wp", 128 * b, "zq", "zs", 0)
            act(r("hs", 240 * b, 240 * b + NS), r(BANKS[b], 0, NS), F.Copy, None, 0.03125)
            tt(r("xt", b, 4 * C, 4), r("hs", 240 * b, 240 * b + 240), r("ff", C * b, C * b + C), A.add, r("el", 0, 18))

    quant("xq3", "xs3", 0, C, r("xt", 0, 4 * C))
    mm("bs", C, "vq", "vs", 0, "xq3", "xs3", 0)
    act(r("yo", 0, C), r("bs", 0, C), F.Copy)
    dma("y", "done", T.oc[:, :], T.xq3[:, 0:C].bitcast(dt.uint8), [r("xq3", 0, C)], [])
    for k in range(4):
        dma("ys"[k % 2], "done", T.osc[4 * k:4 * k + 4, :], T.xs3[32 * k:32 * k + 4, 0:C], [r("xs3", 0, C)], [])
    dma("s", "done", T.y[:, :], T.yo[:, :], [r("yo", 0, C)], [])
    issue()
